import numpy as np
import ml_dtypes


def mxq(x, axis, fmt="e4m3"):
    dtype, down = {"e4m3": (ml_dtypes.float8_e4m3fn, 7), "e5m2": (ml_dtypes.float8_e5m2, 14)}[fmt]
    v = np.moveaxis(np.asarray(x, np.float32).astype(ml_dtypes.bfloat16).astype(np.float64), axis, -1)
    blocks = v.reshape(v.shape[:-1] + (-1, 32))
    amax = np.abs(blocks).max(-1, keepdims=True)
    byte = np.maximum(np.where(amax > 0, np.frexp(amax)[1] - 1 + 127, 0) - down, 1)
    scale = np.exp2(byte - 127.0)
    codes = (blocks / scale).astype(np.float32).astype(dtype).astype(np.float64)
    return np.moveaxis((codes * scale).reshape(v.shape), -1, axis)


WIDE = False


def mx_kscale(k):
    if not WIDE:
        return np.ones(k)
    levels = np.array([10, -10, 5, -5, 0])
    if k % 512:
        return np.exp2(np.random.permutation(np.resize(levels, k // 32))).repeat(32)
    a = np.empty((k // 512, 16))
    for p in range(k // 512):
        a[p, :8] = np.random.permutation(np.resize(levels, 8))
        for g in range(8):
            far = levels[np.abs(levels - a[p, g]) >= 10]
            a[p, g + 8] = far[np.random.randint(len(far))]
    return np.exp2(a.ravel()).repeat(32)


BF16 = ml_dtypes.bfloat16


def bf(x):
    return np.asarray(x, np.float32).astype(BF16)


def f64(x):
    return np.asarray(x).astype(np.float64)


E2M1 = np.array([0.0, 0.5, 1.0, 1.5, 2.0, 3.0, 4.0, 6.0, -0.0, -0.5, -1.0, -1.5, -2.0, -3.0, -4.0, -6.0])


def pack_weight(w, fmt):
    k, n = w.shape
    w = f64(bf(w)).reshape(k // 32, 32, n)
    amax = np.abs(w).max(1)
    if fmt == "e4m3":
        byte = np.frexp(amax)[1] - 1 + 127 - 7
    else:
        mant, ex = np.frexp(amax / 6.0)
        byte = np.where(mant > 0.5, ex, ex - 1) + 127
    byte = np.clip(np.where(amax > 0, byte, 1), 1, 254)
    scaled = (w * np.exp2(127.0 - byte)[:, None, :]).reshape(k, n).astype(np.float32)
    by_word = np.ascontiguousarray(scaled.reshape(k // 512, 128, 4, n).transpose(0, 1, 3, 2))
    if fmt == "e4m3":
        words = by_word.astype(ml_dtypes.float8_e4m3fn).view(np.uint8)
    else:
        c = by_word.astype(ml_dtypes.float4_e2m1fn).view(np.uint8) & 0xF
        words = c[..., 0::2] | (c[..., 1::2] << 4)
    return np.ascontiguousarray(words), np.ascontiguousarray(byte.astype(np.uint8).reshape(k // 512, 16, n))


def unpack_weight(words, scales, fmt):
    g, p, n, _ = words.shape
    if fmt == "e4m3":
        vals = np.ascontiguousarray(words).view(ml_dtypes.float8_e4m3fn).astype(np.float64)
    else:
        nib = np.empty((g, p, n, 4), np.uint8)
        nib[..., 0::2] = words & 0xF
        nib[..., 1::2] = words >> 4
        vals = E2M1[nib]
    vals = vals * np.repeat(np.exp2(scales.astype(np.float64) - 127.0), 8, axis=1)[..., None]
    return vals.transpose(0, 1, 3, 2).reshape(g * 512, n)
def pack4(w):
    words, scales = pack_weight(w, "e2m1")
    return words.reshape(words.shape[0], 128, -1), scales


def unpack4(words, scales):
    return unpack_weight(words.reshape(words.shape[0], 128, -1, 2), scales, "e2m1")


E4M3FN = np.array([(-1.0 if i & 128 else 1.0) * ((1.0 + (i & 7) / 8.0) * 2.0 ** (((i >> 3) & 15) - 7) if i & 120 else (i & 7) * 2.0 ** -9) for i in range(256)])


def e4m3fn_bytes(y):
    return np.clip(np.asarray(y, np.float64), -448.0, 448.0).astype(np.float32).astype(ml_dtypes.float8_e4m3fn).view(np.uint8)


def e4m3fn_values(b):
    return E4M3FN[b]


T, K, F, P, B = 2048, 1024, 1024, 1024, 128


def setup_inputs():
    s = mx_kscale(K)
    u = mx_kscale(T)
    x = np.random.standard_normal((T, K)) * s
    x_scale = (np.abs(x.reshape(T, K // B, B)).max(axis=2) / 448).astype(np.float32)
    x_bytes = e4m3fn_bytes(x / np.repeat(x_scale.astype(np.float64), B, axis=1))
    filt_words, filt_scales = pack4(np.random.standard_normal((T, P)) / np.sqrt(T) / u[:, None])
    return {"x_bytes": x_bytes,
            "x_scale": x_scale,
            "w": bf(np.random.standard_normal((F, K)) / np.sqrt(K) / s),
            "offset": bf(0.5 * np.random.standard_normal(F)),
            "gain": bf((1 + 0.1 * np.random.standard_normal(T)) * u),
            "filt_words": filt_words,
            "filt_scales": filt_scales}


def reference(x_bytes, x_scale, w, offset, gain, filt_words, filt_scales):
    x = e4m3fn_values(x_bytes) * np.repeat(f64(x_scale), B, axis=1)
    y = mxq(x, 1, "e4m3") @ mxq(f64(w), 1, "e4m3").T
    vel = y + f64(offset)
    h = vel * f64(gain)[:, None]
    filt = unpack4(filt_words, filt_scales)
    return filt.T @ mxq(h, 0, "e4m3")

@@ -1,0 +1,358 @@
+from contextlib import ExitStack
+
+import concourse.mybir as mybir
+from concourse.masks import make_identity
+
+T, K, F, P = 2048, 1024, 1024, 1024
+FLOPS = 2 * T * K * F + 2 * T * P * F
+
+F32 = mybir.dt.float32
+BF16 = mybir.dt.bfloat16
+I32 = mybir.dt.int32
+U32 = mybir.dt.uint32
+U8 = mybir.dt.uint8
+FP8 = mybir.dt.float8_e4m3fn
+FP8X4 = mybir.dt.float8_e4m3fn_x4
+FP4X4 = mybir.dt.float4_e2m1fn_x4
+MULT = mybir.AluOpType.mult
+ADD = mybir.AluOpType.add
+COPY = mybir.ActivationFunctionType.Copy
+
+HALF = 512
+PAIRS = 8
+V_BLOCKS = (8, 8, 8, 7, 6, 4, 3, 3)
+OG_ENGINES = "vvvvvvvvssssssss"
+OUT_ENGINES = "ssssssssssssvsvs"
+
+
+def tile_cursor_velocity_filter_d4_kernel(tc, x_bytes, x_scale, w, offset, gain, filt_words, filt_scales, out):
+    nc = tc.nc
+    with ExitStack() as ctx:
+        keep = ctx.enter_context(tc.tile_pool(name="keep", bufs=1))
+        work = ctx.enter_context(tc.tile_pool(name="work", bufs=3))
+        hwork = ctx.enter_context(tc.tile_pool(name="hwork", bufs=2))
+        stage = ctx.enter_context(tc.tile_pool(name="stage", bufs=6))
+        psum = ctx.enter_context(tc.psum_pool(name="psum", bufs=1))
+        ctx.enter_context(tc.manual_schedule())
+
+        def bank(i, name):
+            return psum.tile([128, HALF], F32, name=name, tag=f"bank{i}")
+
+        def u32_tile(cols, name):
+            return keep.tile([128, cols], U32, name=name, align_bytes=64)
+
+        def u8_tile(cols, name):
+            return keep.tile([128, cols], U8, name=name, align_bytes=64)
+
+        off_row = keep.tile([128, F], BF16, name="off_row")
+        nc.vector.memset(off_row[:], 0.0)
+        ones = keep.tile([128, 128], BF16, name="ones")
+        nc.vector.memset(ones[:], 1.0)
+        ident = keep.tile([128, 128], F32, name="ident")
+        make_identity(nc, ident[:])
+        fs = u8_tile(4 * P, "fs")
+        nc.gpsimd.memset(fs[:].bitcast(I32), 0)
+
+        gain_bf = keep.tile([128, 4, 4], BF16, name="gain_bf")
+        nc.scalar.dma_start(out=gain_bf[:], in_=gain.rearrange("(g p t) -> p g t", p=128, t=4))
+        nc.scalar.dma_start(out=off_row[0:1, :], in_=offset.unsqueeze(0))
+
+        xs = keep.tile([128, 4, 32], F32, name="xs")
+        nc.sync.dma_start(out=xs[:], in_=x_scale.rearrange("(g p t) j -> p g (t j)", p=128, t=4))
+        x_view = x_bytes.rearrange("(g p t) k -> g p (t k)", p=128, t=4)
+        xb = [keep.tile([128, 4 * K], U8, name=f"xb{g}", align_bytes=64) for g in range(4)]
+        wr = [keep.tile([128, K], BF16, name=f"wr{r}", align_bytes=64) for r in range(8)]
+
+        def load_w(r):
+            nc.sync.dma_start(out=wr[r][:], in_=w[128 * r : 128 * r + 128, :])
+
+        nc.sync.dma_start(out=xb[0][:, 0 : 2 * K], in_=x_view[0][:, 0 : 2 * K])
+        load_w(0)
+        load_w(1)
+        nc.sync.dma_start(out=xb[0][:, 2 * K : 4 * K], in_=x_view[0][:, 2 * K : 4 * K])
+        load_w(2)
+        load_w(3)
+        for g in range(1, 4):
+            nc.sync.dma_start(out=xb[g][:], in_=x_view[g])
+        for r in range(4, 8):
+            load_w(r)
+        fw = u8_tile(4 * 2 * P, "fw")
+        nc.sync.dma_start(
+            out=fw[:].bitcast(I32).rearrange("p (g c) -> p g c", g=4),
+            in_=filt_words.bitcast(I32).rearrange("g p c -> p g c"),
+        )
+        for q in range(4):
+            nc.sync.dma_start(
+                out=fs[32 * q : 32 * q + 4, :].bitcast(I32).rearrange("q (g n) -> q g n", g=4),
+                in_=filt_scales.bitcast(I32)[:, 4 * q : 4 * q + 4, :].rearrange("g q n -> q g n"),
+            )
+
+        gain_f = keep.tile([128, 16], F32, name="gain_f")
+        nc.scalar.copy(out=gain_f[:], in_=gain_bf[:].rearrange("p g t -> p (g t)"))
+
+        off_all = keep.tile([128, F], BF16, name="off_all")
+        for h in range(2):
+            ob = bank(4 + h, f"ob{h}")
+            nc.tensor.matmul(ob[:], lhsT=ones[:], rhs=off_row[:, HALF * h : HALF * h + HALF], start=True, stop=True)
+            if h == 0:
+                nc.vector.tensor_copy(out=off_all[:, 0:HALF], in_=ob[:])
+            else:
+                nc.scalar.copy(out=off_all[:, HALF:F], in_=ob[:])
+
+        xw = {}
+        xg = {}
+        xc = {}
+        xsc = {}
+        banks = {}
+
+        def widen(k, part=None):
+            g, h = divmod(k, 2)
+            if part in (None, 0):
+                xw[k] = work.tile([128, 2 * K], BF16, name=f"xw{k}", tag="xw", align_bytes=64)
+            nv = V_BLOCKS[k]
+            blocks = range(16) if part is None else range(8 * part, 8 * part + 8)
+            for b in blocks:
+                src = xb[g][:, 2 * K * h + 128 * b : 2 * K * h + 128 * b + 128].bitcast(FP8)
+                dst = xw[k][:, 128 * b : 128 * b + 128]
+                sc = xs[:, g, 16 * h + b : 16 * h + b + 1]
+                if (b + 1) * nv // 16 > b * nv // 16:
+                    nc.vector.tensor_scalar(out=dst, in0=src, scalar1=sc, scalar2=None, op0=MULT)
+                else:
+                    nc.scalar.activation(out=dst, in_=src, func=COPY, scale=sc)
+
+        def turn(words, b):
+            for g in range(2):
+                for u in range(2):
+                    c = 2 * g + u
+                    nc.tensor.transpose(b[:, 128 * c : 128 * c + 128], words[:, 256 * g + u : 256 * g + 256 : 2], ident[:])
+
+        def turn_x(k, b0):
+            words = xw[k][:].bitcast(F32)
+            banks["x", k] = [bank(b0 + t, f"xt{k}_{t}") for t in range(2)]
+            for t in range(2):
+                turn(words[:, 512 * t : 512 * t + 512], banks["x", k][t])
+
+        def take(engine, dst, b):
+            src = b[:].rearrange("p (g u r) -> p g r u", g=2, u=2)
+            if engine == "s":
+                nc.scalar.copy(out=dst, in_=src)
+            else:
+                nc.vector.tensor_copy(out=dst, in_=src)
+
+        def empty_x(k, t, engine):
+            if t == 0:
+                xg[k] = work.tile([128, 2, 2, 128, 4], BF16, name=f"xg{k}", tag="xg", align_bytes=64)
+            dst = xg[k][:].rearrange("p a g r v -> p (a g r v)").bitcast(F32)[:, 512 * t : 512 * t + 512]
+            take(engine, dst.rearrange("p (g r u) -> p g r u", g=2, u=2), banks["x", k][t])
+
+        def quant_x(k):
+            xc[k] = u32_tile(512, f"xc{k}")
+            xsc[k] = u8_tile(512, f"xsc{k}")
+            nc.vector.quantize_mx(
+                out=xc[k][:].bitcast(FP8X4), scales=xsc[k][:], in_=xg[k][:].rearrange("p a g r v -> p (a g r v)")
+            )
+
+        wg = {}
+        wc = {}
+        wsc = {}
+
+        def turn_w(j, b0):
+            banks["w", j] = [bank(b0 + t, f"wt{j}_{t}") for t in range(2)]
+            for t in range(2):
+                turn(wr[2 * j + t][:].bitcast(F32), banks["w", j][t])
+
+        def empty_w(j, t, engine):
+            if t == 0:
+                wg[j] = work.tile([128, 2, 256, 4], BF16, name=f"wg{j}", tag="wg", bufs=2, align_bytes=64)
+            dst = wg[j][:].rearrange("p g r v -> p (g r v)").bitcast(F32).rearrange("p (g r u) -> p g r u", g=2, u=2)
+            take(engine, dst[:, :, 128 * t : 128 * t + 128, :], banks["w", j][t])
+
+        def quant_w(j):
+            h, q = divmod(j, 2)
+            if q == 0:
+                wc[h] = u32_tile(2 * HALF, f"wc{h}")
+                wsc[h] = u8_tile(2 * HALF, f"wsc{h}")
+            for g in range(2):
+                c = slice(HALF * g + 256 * q, HALF * g + 256 * q + 256)
+                nc.vector.quantize_mx(
+                    out=wc[h][:, c].bitcast(FP8X4), scales=wsc[h][:, c], in_=wg[j][:, g, :, :].rearrange("p r v -> p (r v)")
+                )
+
+        og = {}
+        hp = {}
+        hg = {}
+        hc = {}
+        hsc = {}
+
+        def make_og(m):
+            h, k = divmod(m, PAIRS)
+            og[m] = work.tile([128, 2, HALF], F32, name=f"og{m}", tag="og", bufs=10)
+            for t in range(2):
+                i = 2 * k + t
+                src = off_all[:, HALF * h : HALF * h + HALF]
+                if OG_ENGINES[m] == "s":
+                    nc.scalar.activation(out=og[m][:, t, :], in_=src, func=COPY, scale=gain_f[:, i : i + 1])
+                else:
+                    nc.vector.tensor_scalar(
+                        out=og[m][:, t, :], in0=src, scalar1=gain_f[:, i : i + 1], scalar2=None, op0=MULT
+                    )
+
+        def first(m):
+            h, k = divmod(m, PAIRS)
+            banks["y", m] = [bank(2 + t, f"y{m}_{t}") for t in range(2)]
+            for t in range(2):
+                for g in range(2):
+                    c = 128 * (2 * t + g)
+                    nc.tensor.matmul_mx(
+                        out=banks["y", m][t][:],
+                        lhsT=xc[k][:, c : c + 128].bitcast(FP8X4),
+                        lhsT_scale=xsc[k][:, c : c + 128],
+                        rhs=wc[h][:, HALF * g : HALF * g + HALF].bitcast(FP8X4),
+                        rhs_scale=wsc[h][:, HALF * g : HALF * g + HALF],
+                        start=(g == 0),
+                        stop=(g == 1),
+                    )
+
+        def finish(m, t):
+            h, k = divmod(m, PAIRS)
+            big, q = divmod(m, 2)
+            if q == 0 and t == 0:
+                hp[big] = hwork.tile([128, 4, HALF], BF16, name=f"hp{big}", tag="hp", align_bytes=64)
+            i = 2 * k + t
+            nc.vector.scalar_tensor_tensor(
+                out=hp[big][:, 2 * q + t, :],
+                in0=banks["y", m][t][:],
+                scalar=gain_f[:, i : i + 1],
+                in1=og[m][:, t, :],
+                op0=MULT,
+                op1=ADD,
+            )
+
+        def weave(big, first_col, last_col, engine):
+            if first_col == 0:
+                hg[big] = hwork.tile([128, HALF, 4], BF16, name=f"hg{big}", tag="hg", align_bytes=64)
+            c = slice(first_col, last_col)
+            dst, src = hg[big][:, c, :], hp[big][:, :, c].rearrange("p t n -> p n t")
+            if engine == "s":
+                nc.scalar.copy(out=dst, in_=src)
+            else:
+                nc.vector.tensor_copy(out=dst, in_=src)
+
+        def quant_h(big):
+            hc[big] = u32_tile(HALF, f"hc{big}")
+            hsc[big] = u8_tile(HALF, f"hsc{big}")
+            nc.vector.quantize_mx(
+                out=hc[big][:].bitcast(FP8X4), scales=hsc[big][:], in_=hg[big][:].rearrange("p n t -> p (n t)")
+            )
+
+        acc = {}
+        where = {(0, 0): 4, (0, 1): 5, (0, 2): 6, (0, 3): 7, (0, 4): 0, (0, 5): 1, (0, 6): 4, (0, 7): 5,
+                 (1, 0): 6, (1, 1): 7, (1, 2): 0, (1, 3): 1, (1, 4): 4, (1, 5): 5, (1, 6): 2, (1, 7): 3}
+
+        def second(h, pt, g):
+            if g == 0:
+                acc[h, pt] = bank(where[h, pt], f"acc{h}_{pt}")
+            big = 4 * h + g
+            nc.tensor.matmul_mx(
+                out=acc[h, pt][:],
+                lhsT=fw[:, 2 * P * g + 256 * pt : 2 * P * g + 256 * pt + 256].bitcast(FP4X4),
+                lhsT_scale=fs[:, P * g + 128 * pt : P * g + 128 * pt + 128],
+                rhs=hc[big][:].bitcast(FP8X4),
+                rhs_scale=hsc[big][:],
+                start=(g == 0),
+                stop=(g == 3),
+            )
+
+        def store(h, pt):
+            res = stage.tile([128, HALF], F32, name=f"res{h}_{pt}", tag="res")
+            if OUT_ENGINES[8 * h + pt] == "s":
+                nc.scalar.copy(out=res[:], in_=acc[h, pt][:])
+            else:
+                nc.vector.tensor_copy(out=res[:], in_=acc[h, pt][:])
+            nc.sync.dma_start(out=out[128 * pt : 128 * pt + 128, HALF * h : HALF * h + HALF], in_=res[:])
+
+        widen(0)
+        make_og(0)
+        turn_w(0, 0)
+        empty_w(0, 0, "s")
+        empty_w(0, 1, "v")
+        turn_x(0, 6)
+        quant_w(0)
+        turn_w(1, 2)
+        empty_x(0, 0, "s")
+        empty_x(0, 1, "v")
+        widen(1, 0)
+        empty_w(1, 0, "s")
+        empty_w(1, 1, "v")
+        quant_x(0)
+        widen(1, 1)
+        quant_w(1)
+        turn_x(1, 4)
+        make_og(1)
+        empty_x(1, 0, "s")
+        empty_x(1, 1, "v")
+        widen(2)
+        make_og(2)
+
+        plan = {
+            4: [(0, 0, 0), (0, 1, 0)], 5: [(0, 2, 0), (0, 3, 0)],
+            6: [(0, 0, 1), (0, 1, 1)], 7: [(0, 2, 1), (0, 3, 1)],
+            8: [(0, 0, 2), (0, 1, 2), (0, 4, 0), (0, 4, 1), (0, 4, 2)],
+            9: [(0, 2, 2), (0, 3, 2), (0, 5, 0), (0, 5, 1), (0, 5, 2)],
+            10: [(0, pt, 3) for pt in range(6)],
+            11: [(0, pt, g) for pt in (6, 7) for g in range(4)],
+            12: [(1, pt, 0) for pt in range(4)],
+            13: [(1, pt, 0) for pt in (4, 5)],
+            14: [(1, pt, 1) for pt in range(4)],
+            15: [(1, pt, 1) for pt in (4, 5)],
+            16: [(1, pt, 2) for pt in range(6)],
+            17: [(1, pt, g) for pt in (6, 7) for g in range(3)],
+            18: [(1, pt, 3) for pt in (0, 1, 2, 3, 4, 5, 6, 7)],
+        }
+
+        for s in range(19):
+            if s == 0:
+                first(0)
+            if s + 2 < PAIRS:
+                turn_x(s + 2, 0)
+            if s in (6, 7):
+                turn_w(s - 4, 0)
+            if s + 3 < PAIRS:
+                widen(s + 3, 0)
+            old = (s - 3) // 2
+            if 1 <= s <= 16:
+                finish(s - 1, 0)
+            if s % 2 == 0 and s >= 4 and s < 18:
+                quant_h((s - 4) // 2)
+            if s % 2 == 1 and 3 <= s < 17:
+                weave(old, 0, 256, "v")
+            if 1 <= s <= 16:
+                finish(s - 1, 1)
+            if s % 2 == 1 and 3 <= s < 17:
+                weave(old, 256, 512, "v")
+            if s + 2 < PAIRS:
+                empty_x(s + 2, 0, "s")
+            if s in (6, 7):
+                empty_w(s - 4, 0, "s")
+            if s + 3 < PAIRS:
+                widen(s + 3, 1)
+            if s + 2 < PAIRS:
+                empty_x(s + 2, 1, "s")
+            if s in (6, 7):
+                empty_w(s - 4, 1, "s")
+            if s + 1 < PAIRS:
+                quant_x(s + 1)
+            if s in (6, 7):
+                quant_w(s - 4)
+            if s < 13:
+                make_og(s + 3)
+            if 1 <= s < 16:
+                first(s)
+            if s == 17:
+                weave(7, 0, 384, "v")
+                weave(7, 384, 512, "s")
+                quant_h(7)
+            for task in plan.get(s, []):
+                second(*task)
+                if task[2] == 3:
+                    store(task[0], task[1])

@@ -20,9 +20,16 @@ COPY = mybir.ActivationFunctionType.Copy
 
 HALF = 512
 PAIRS = 8
-V_BLOCKS = (8, 8, 8, 7, 6, 4, 3, 3)
-OG_ENGINES = "vvvvvvvvssssssss"
-OUT_ENGINES = "ssssssssssssvsvs"
+V_BLOCKS = (16, 16, 7, 4, 5, 5, 6, 3)
+OG_ENGINES = "vvvvvvvssssssvvv"
+OUT_ENGINES = "ssssssssssssssss"
+X_ENGINES = "sssvssssssssvsss"
+W_ENGINES = "ssssssss"
+WEAVE_ENGINES = "vvvssvvsvvsvvv"
+TAIL_COLS = 384
+WARM = 10
+W_STEPS = (1, 2)
+WARM_HEAD = 2
 
 
 def tile_cursor_velocity_filter_d4_kernel(tc, x_bytes, x_scale, w, offset, gain, filt_words, filt_scales, out):
@@ -44,6 +51,9 @@ def tile_cursor_velocity_filter_d4_kernel(tc, x_bytes, x_scale, w, offset, gain,
         def u8_tile(cols, name):
             return keep.tile([128, cols], U8, name=name, align_bytes=64)
 
+        zeros = keep.tile([128, HALF], BF16, name="zeros")
+        nc.vector.memset(zeros[:], 0.0)
+        spare = bank(3, "spare")
         off_row = keep.tile([128, F], BF16, name="off_row")
         nc.vector.memset(off_row[:], 0.0)
         ones = keep.tile([128, 128], BF16, name="ones")
@@ -90,6 +100,9 @@ def tile_cursor_velocity_filter_d4_kernel(tc, x_bytes, x_scale, w, offset, gain,
         gain_f = keep.tile([128, 16], F32, name="gain_f")
         nc.scalar.copy(out=gain_f[:], in_=gain_bf[:].rearrange("p g t -> p (g t)"))
 
+        for i in range(WARM):
+            nc.tensor.matmul(spare[:], lhsT=zeros[:, 0:128], rhs=zeros[:], start=True, stop=True)
+
         off_all = keep.tile([128, F], BF16, name="off_all")
         for h in range(2):
             ob = bank(4 + h, f"ob{h}")
@@ -126,6 +139,12 @@ def tile_cursor_velocity_filter_d4_kernel(tc, x_bytes, x_scale, w, offset, gain,
                     c = 2 * g + u
                     nc.tensor.transpose(b[:, 128 * c : 128 * c + 128], words[:, 256 * g + u : 256 * g + 256 : 2], ident[:])
 
+        def keep_warm(b):
+            if WARM_HEAD:
+                idle = bank(b, f"idle{b}")
+                for i in range(WARM_HEAD):
+                    nc.tensor.matmul(idle[:], lhsT=zeros[:, 0:128], rhs=zeros[:], start=True, stop=True)
+
         def turn_x(k, b0):
             words = xw[k][:].bitcast(F32)
             banks["x", k] = [bank(b0 + t, f"xt{k}_{t}") for t in range(2)]
@@ -139,11 +158,11 @@ def tile_cursor_velocity_filter_d4_kernel(tc, x_bytes, x_scale, w, offset, gain,
             else:
                 nc.vector.tensor_copy(out=dst, in_=src)
 
-        def empty_x(k, t, engine):
+        def empty_x(k, t):
             if t == 0:
                 xg[k] = work.tile([128, 2, 2, 128, 4], BF16, name=f"xg{k}", tag="xg", align_bytes=64)
             dst = xg[k][:].rearrange("p a g r v -> p (a g r v)").bitcast(F32)[:, 512 * t : 512 * t + 512]
-            take(engine, dst.rearrange("p (g r u) -> p g r u", g=2, u=2), banks["x", k][t])
+            take(X_ENGINES[2 * k + t], dst.rearrange("p (g r u) -> p g r u", g=2, u=2), banks["x", k][t])
 
         def quant_x(k):
             xc[k] = u32_tile(512, f"xc{k}")
@@ -161,11 +180,11 @@ def tile_cursor_velocity_filter_d4_kernel(tc, x_bytes, x_scale, w, offset, gain,
             for t in range(2):
                 turn(wr[2 * j + t][:].bitcast(F32), banks["w", j][t])
 
-        def empty_w(j, t, engine):
+        def empty_w(j, t):
             if t == 0:
                 wg[j] = work.tile([128, 2, 256, 4], BF16, name=f"wg{j}", tag="wg", bufs=2, align_bytes=64)
             dst = wg[j][:].rearrange("p g r v -> p (g r v)").bitcast(F32).rearrange("p (g r u) -> p g r u", g=2, u=2)
-            take(engine, dst[:, :, 128 * t : 128 * t + 128, :], banks["w", j][t])
+            take(W_ENGINES[2 * j + t], dst[:, :, 128 * t : 128 * t + 128, :], banks["w", j][t])
 
         def quant_w(j):
             h, q = divmod(j, 2)
@@ -274,31 +293,33 @@ def tile_cursor_velocity_filter_d4_kernel(tc, x_bytes, x_scale, w, offset, gain,
         widen(0)
         make_og(0)
         turn_w(0, 0)
-        empty_w(0, 0, "s")
-        empty_w(0, 1, "v")
+        empty_w(0, 0)
+        empty_w(0, 1)
+        keep_warm(4)
         turn_x(0, 6)
         quant_w(0)
+        keep_warm(5)
         turn_w(1, 2)
-        empty_x(0, 0, "s")
-        empty_x(0, 1, "v")
+        empty_x(0, 0)
+        empty_x(0, 1)
         widen(1, 0)
-        empty_w(1, 0, "s")
-        empty_w(1, 1, "v")
+        empty_w(1, 0)
+        empty_w(1, 1)
         quant_x(0)
         widen(1, 1)
         quant_w(1)
         turn_x(1, 4)
         make_og(1)
-        empty_x(1, 0, "s")
-        empty_x(1, 1, "v")
+        empty_x(1, 0)
+        empty_x(1, 1)
         widen(2)
         make_og(2)
 
         plan = {
             4: [(0, 0, 0), (0, 1, 0)], 5: [(0, 2, 0), (0, 3, 0)],
-            6: [(0, 0, 1), (0, 1, 1)], 7: [(0, 2, 1), (0, 3, 1)],
-            8: [(0, 0, 2), (0, 1, 2), (0, 4, 0), (0, 4, 1), (0, 4, 2)],
-            9: [(0, 2, 2), (0, 3, 2), (0, 5, 0), (0, 5, 1), (0, 5, 2)],
+            6: [(0, 0, 1), (0, 1, 1), (0, 4, 0), (0, 4, 1)], 7: [(0, 2, 1), (0, 3, 1), (0, 5, 0), (0, 5, 1)],
+            8: [(0, 0, 2), (0, 1, 2), (0, 2, 2)],
+            9: [(0, 3, 2), (0, 4, 2), (0, 5, 2)],
             10: [(0, pt, 3) for pt in range(6)],
             11: [(0, pt, g) for pt in (6, 7) for g in range(4)],
             12: [(1, pt, 0) for pt in range(4)],
@@ -315,8 +336,9 @@ def tile_cursor_velocity_filter_d4_kernel(tc, x_bytes, x_scale, w, offset, gain,
                 first(0)
             if s + 2 < PAIRS:
                 turn_x(s + 2, 0)
-            if s in (6, 7):
-                turn_w(s - 4, 0)
+            if s - 1 in W_STEPS:
+                empty_w(s - 1 - W_STEPS[0] + 2, 0)
+                empty_w(s - 1 - W_STEPS[0] + 2, 1)
             if s + 3 < PAIRS:
                 widen(s + 3, 0)
             old = (s - 3) // 2
@@ -325,32 +347,30 @@ def tile_cursor_velocity_filter_d4_kernel(tc, x_bytes, x_scale, w, offset, gain,
             if s % 2 == 0 and s >= 4 and s < 18:
                 quant_h((s - 4) // 2)
             if s % 2 == 1 and 3 <= s < 17:
-                weave(old, 0, 256, "v")
+                weave(old, 0, 256, WEAVE_ENGINES[2 * old])
             if 1 <= s <= 16:
                 finish(s - 1, 1)
             if s % 2 == 1 and 3 <= s < 17:
-                weave(old, 256, 512, "v")
+                weave(old, 256, 512, WEAVE_ENGINES[2 * old + 1])
             if s + 2 < PAIRS:
-                empty_x(s + 2, 0, "s")
-            if s in (6, 7):
-                empty_w(s - 4, 0, "s")
+                empty_x(s + 2, 0)
             if s + 3 < PAIRS:
                 widen(s + 3, 1)
             if s + 2 < PAIRS:
-                empty_x(s + 2, 1, "s")
-            if s in (6, 7):
-                empty_w(s - 4, 1, "s")
+                empty_x(s + 2, 1)
             if s + 1 < PAIRS:
                 quant_x(s + 1)
-            if s in (6, 7):
-                quant_w(s - 4)
+            if s in (5, 6):
+                quant_w(s - 3)
             if s < 13:
                 make_og(s + 3)
             if 1 <= s < 16:
                 first(s)
+            if s in W_STEPS:
+                turn_w(s - W_STEPS[0] + 2, 4 + 2 * (s - W_STEPS[0]))
             if s == 17:
-                weave(7, 0, 384, "v")
-                weave(7, 384, 512, "s")
+                weave(7, 0, TAIL_COLS, "v")
+                weave(7, TAIL_COLS, 512, "s")
                 quant_h(7)
             for task in plan.get(s, []):
                 second(*task)

@@ -20,13 +20,14 @@ COPY = mybir.ActivationFunctionType.Copy
 
 HALF = 512
 PAIRS = 8
-V_BLOCKS = (16, 16, 7, 4, 5, 5, 6, 3)
-OG_ENGINES = "vvvvvvvssssssvvv"
+V_BLOCKS = (16, 16, 6, 4, 5, 6, 6, 3)
+OG_ENGINES = "vvvvvvvssssssvss"
 OUT_ENGINES = "ssssssssssssssss"
 X_ENGINES = "sssvssssssssvsss"
 W_ENGINES = "ssssssss"
-WEAVE_ENGINES = "vvvssvvsvvsvvv"
+WEAVE_ENGINES = "vvvssvvsvvvvvv"
 TAIL_COLS = 384
+X_BANKS = (6, 4, 0, 4, 0, 6, 0, 0)
 WARM = 10
 W_STEPS = (1, 2)
 WARM_HEAD = 2
@@ -63,12 +64,14 @@ def tile_cursor_velocity_filter_d4_kernel(tc, x_bytes, x_scale, w, offset, gain,
         fs = u8_tile(4 * P, "fs")
         nc.gpsimd.memset(fs[:].bitcast(I32), 0)
 
-        gain_bf = keep.tile([128, 4, 4], BF16, name="gain_bf")
-        nc.scalar.dma_start(out=gain_bf[:], in_=gain.rearrange("(g p t) -> p g t", p=128, t=4))
+        gain_rows = keep.tile([128, 512], BF16, name="gain_rows")
+        nc.vector.memset(gain_rows[:], 0.0)
         nc.scalar.dma_start(out=off_row[0:1, :], in_=offset.unsqueeze(0))
+        nc.scalar.dma_start(out=gain_rows[0:4, :], in_=gain.rearrange("(g c) -> g c", g=4))
 
         xs = keep.tile([128, 4, 32], F32, name="xs")
-        nc.sync.dma_start(out=xs[:], in_=x_scale.rearrange("(g p t) j -> p g (t j)", p=128, t=4))
+        xs_view = x_scale.rearrange("(g p t) j -> p g (t j)", p=128, t=4)
+        nc.sync.dma_start(out=xs[:, 0, :], in_=xs_view[:, 0, :])
         x_view = x_bytes.rearrange("(g p t) k -> g p (t k)", p=128, t=4)
         xb = [keep.tile([128, 4 * K], U8, name=f"xb{g}", align_bytes=64) for g in range(4)]
         wr = [keep.tile([128, K], BF16, name=f"wr{r}", align_bytes=64) for r in range(8)]
@@ -82,6 +85,7 @@ def tile_cursor_velocity_filter_d4_kernel(tc, x_bytes, x_scale, w, offset, gain,
         nc.sync.dma_start(out=xb[0][:, 2 * K : 4 * K], in_=x_view[0][:, 2 * K : 4 * K])
         load_w(2)
         load_w(3)
+        nc.sync.dma_start(out=xs[:, 1:4, :], in_=xs_view[:, 1:4, :])
         for g in range(1, 4):
             nc.sync.dma_start(out=xb[g][:], in_=x_view[g])
         for r in range(4, 8):
@@ -98,7 +102,8 @@ def tile_cursor_velocity_filter_d4_kernel(tc, x_bytes, x_scale, w, offset, gain,
             )
 
         gain_f = keep.tile([128, 16], F32, name="gain_f")
-        nc.scalar.copy(out=gain_f[:], in_=gain_bf[:].rearrange("p g t -> p (g t)"))
+        ident_bf = keep.tile([128, 4], BF16, name="ident_bf")
+        nc.vector.tensor_copy(out=ident_bf[:], in_=ident[:, 0:4])
 
         for i in range(WARM):
             nc.tensor.matmul(spare[:], lhsT=zeros[:, 0:128], rhs=zeros[:], start=True, stop=True)
@@ -111,6 +116,12 @@ def tile_cursor_velocity_filter_d4_kernel(tc, x_bytes, x_scale, w, offset, gain,
                 nc.vector.tensor_copy(out=off_all[:, 0:HALF], in_=ob[:])
             else:
                 nc.scalar.copy(out=off_all[:, HALF:F], in_=ob[:])
+        gb = bank(2, "gb")
+        for t in range(4):
+            nc.tensor.matmul(gb[:, 4 * t : 4 * t + 4], lhsT=gain_rows[:, t:512:4], rhs=ident_bf[:], start=True, stop=True)
+        nc.vector.tensor_copy(
+            out=gain_f[:].rearrange("p (g t) -> p g t", g=4), in_=gb[:, 0:16].rearrange("p (t g) -> p g t", t=4)
+        )
 
         xw = {}
         xg = {}
@@ -145,7 +156,8 @@ def tile_cursor_velocity_filter_d4_kernel(tc, x_bytes, x_scale, w, offset, gain,
                 for i in range(WARM_HEAD):
                     nc.tensor.matmul(idle[:], lhsT=zeros[:, 0:128], rhs=zeros[:], start=True, stop=True)
 
-        def turn_x(k, b0):
+        def turn_x(k):
+            b0 = X_BANKS[k]
             words = xw[k][:].bitcast(F32)
             banks["x", k] = [bank(b0 + t, f"xt{k}_{t}") for t in range(2)]
             for t in range(2):
@@ -295,8 +307,7 @@ def tile_cursor_velocity_filter_d4_kernel(tc, x_bytes, x_scale, w, offset, gain,
         turn_w(0, 0)
         empty_w(0, 0)
         empty_w(0, 1)
-        keep_warm(4)
-        turn_x(0, 6)
+        turn_x(0)
         quant_w(0)
         keep_warm(5)
         turn_w(1, 2)
@@ -308,7 +319,7 @@ def tile_cursor_velocity_filter_d4_kernel(tc, x_bytes, x_scale, w, offset, gain,
         quant_x(0)
         widen(1, 1)
         quant_w(1)
-        turn_x(1, 4)
+        turn_x(1)
         make_og(1)
         empty_x(1, 0)
         empty_x(1, 1)
@@ -321,11 +332,11 @@ def tile_cursor_velocity_filter_d4_kernel(tc, x_bytes, x_scale, w, offset, gain,
             8: [(0, 0, 2), (0, 1, 2), (0, 2, 2)],
             9: [(0, 3, 2), (0, 4, 2), (0, 5, 2)],
             10: [(0, pt, 3) for pt in range(6)],
-            11: [(0, pt, g) for pt in (6, 7) for g in range(4)],
-            12: [(1, pt, 0) for pt in range(4)],
-            13: [(1, pt, 0) for pt in (4, 5)],
+            11: [(0, 6, g) for g in range(4)],
+            12: [(0, 7, g) for g in range(4)],
+            13: [(1, pt, 0) for pt in range(4)],
             14: [(1, pt, 1) for pt in range(4)],
-            15: [(1, pt, 1) for pt in (4, 5)],
+            15: [(1, pt, g) for pt in (4, 5) for g in range(2)],
             16: [(1, pt, 2) for pt in range(6)],
             17: [(1, pt, g) for pt in (6, 7) for g in range(3)],
             18: [(1, pt, 3) for pt in (0, 1, 2, 3, 4, 5, 6, 7)],
@@ -335,7 +346,7 @@ def tile_cursor_velocity_filter_d4_kernel(tc, x_bytes, x_scale, w, offset, gain,
             if s == 0:
                 first(0)
             if s + 2 < PAIRS:
-                turn_x(s + 2, 0)
+                turn_x(s + 2)
             if s - 1 in W_STEPS:
                 empty_w(s - 1 - W_STEPS[0] + 2, 0)
                 empty_w(s - 1 - W_STEPS[0] + 2, 1)
@@ -367,7 +378,7 @@ def tile_cursor_velocity_filter_d4_kernel(tc, x_bytes, x_scale, w, offset, gain,
             if 1 <= s < 16:
                 first(s)
             if s in W_STEPS:
-                turn_w(s - W_STEPS[0] + 2, 4 + 2 * (s - W_STEPS[0]))
+                turn_w(s - W_STEPS[0] + 2, 6 - 2 * (s - W_STEPS[0]))
             if s == 17:
                 weave(7, 0, TAIL_COLS, "v")
                 weave(7, TAIL_COLS, 512, "s")

@@ -20,16 +20,18 @@ COPY = mybir.ActivationFunctionType.Copy
 
 HALF = 512
 PAIRS = 8
-V_BLOCKS = (16, 16, 6, 4, 5, 6, 6, 3)
-OG_ENGINES = "vvvvvvvssssssvss"
+V_BLOCKS = (8, 8, 8, 7, 7, 0, 2, 0, 3, 2, 8, 0, 6, 0, 3, 0)
+OG_ENGINES = "vvvvvvvssvsvssss"
 OUT_ENGINES = "ssssssssssssssss"
-X_ENGINES = "sssvssssssssvsss"
+X_ENGINES = "sssvsssssssssvss"
 W_ENGINES = "ssssssss"
-WEAVE_ENGINES = "vvvssvvsvvvvvv"
+WEAVE_ENGINES = "vvvssssvvvvvvv"
 TAIL_COLS = 384
-X_BANKS = (6, 4, 0, 4, 0, 6, 0, 0)
+OG_LEAD = 1
+X_BANKS = (6, 4, 0, 4, 0, 4, 4, 0)
+W_BANKS = (0, 2, 6, 0)
 WARM = 10
-W_STEPS = (1, 2)
+W_STEPS = (2, 3)
 WARM_HEAD = 2
 
 
@@ -39,7 +41,7 @@ def tile_cursor_velocity_filter_d4_kernel(tc, x_bytes, x_scale, w, offset, gain,
         keep = ctx.enter_context(tc.tile_pool(name="keep", bufs=1))
         work = ctx.enter_context(tc.tile_pool(name="work", bufs=3))
         hwork = ctx.enter_context(tc.tile_pool(name="hwork", bufs=2))
-        stage = ctx.enter_context(tc.tile_pool(name="stage", bufs=6))
+        stage = ctx.enter_context(tc.tile_pool(name="stage", bufs=10))
         psum = ctx.enter_context(tc.psum_pool(name="psum", bufs=1))
         ctx.enter_context(tc.manual_schedule())
 
@@ -109,19 +111,14 @@ def tile_cursor_velocity_filter_d4_kernel(tc, x_bytes, x_scale, w, offset, gain,
             nc.tensor.matmul(spare[:], lhsT=zeros[:, 0:128], rhs=zeros[:], start=True, stop=True)
 
         off_all = keep.tile([128, F], BF16, name="off_all")
+        obs = []
         for h in range(2):
             ob = bank(4 + h, f"ob{h}")
             nc.tensor.matmul(ob[:], lhsT=ones[:], rhs=off_row[:, HALF * h : HALF * h + HALF], start=True, stop=True)
-            if h == 0:
-                nc.vector.tensor_copy(out=off_all[:, 0:HALF], in_=ob[:])
-            else:
-                nc.scalar.copy(out=off_all[:, HALF:F], in_=ob[:])
+            obs.append(ob)
         gb = bank(2, "gb")
         for t in range(4):
             nc.tensor.matmul(gb[:, 4 * t : 4 * t + 4], lhsT=gain_rows[:, t:512:4], rhs=ident_bf[:], start=True, stop=True)
-        nc.vector.tensor_copy(
-            out=gain_f[:].rearrange("p (g t) -> p g t", g=4), in_=gb[:, 0:16].rearrange("p (t g) -> p g t", t=4)
-        )
 
         xw = {}
         xg = {}
@@ -133,22 +130,31 @@ def tile_cursor_velocity_filter_d4_kernel(tc, x_bytes, x_scale, w, offset, gain,
             g, h = divmod(k, 2)
             if part in (None, 0):
                 xw[k] = work.tile([128, 2 * K], BF16, name=f"xw{k}", tag="xw", align_bytes=64)
-            nv = V_BLOCKS[k]
             blocks = range(16) if part is None else range(8 * part, 8 * part + 8)
             for b in blocks:
                 src = xb[g][:, 2 * K * h + 128 * b : 2 * K * h + 128 * b + 128].bitcast(FP8)
                 dst = xw[k][:, 128 * b : 128 * b + 128]
                 sc = xs[:, g, 16 * h + b : 16 * h + b + 1]
-                if (b + 1) * nv // 16 > b * nv // 16:
+                t, j = divmod(b, 8)
+                nv = V_BLOCKS[2 * k + t]
+                if nv == 8:
+                    by_u = xw[k][:, K * t : K * t + K].rearrange("x (g u p e) -> x g p u e", g=2, u=2, e=2)
+                    dst = by_u[:, j // 4, 32 * (j % 4) : 32 * (j % 4) + 32, :, :]
+                    src = src.rearrange("x (p u e) -> x p u e", u=2, e=2)
+                if (j + 1) * nv // 8 > j * nv // 8:
                     nc.vector.tensor_scalar(out=dst, in0=src, scalar1=sc, scalar2=None, op0=MULT)
                 else:
                     nc.scalar.activation(out=dst, in_=src, func=COPY, scale=sc)
 
-        def turn(words, b):
+        def turn(words, b, by_u=False):
             for g in range(2):
                 for u in range(2):
                     c = 2 * g + u
-                    nc.tensor.transpose(b[:, 128 * c : 128 * c + 128], words[:, 256 * g + u : 256 * g + 256 : 2], ident[:])
+                    if by_u:
+                        part = words[:, 128 * c : 128 * c + 128]
+                    else:
+                        part = words[:, 256 * g + u : 256 * g + 256 : 2]
+                    nc.tensor.transpose(b[:, 128 * c : 128 * c + 128], part, ident[:])
 
         def keep_warm(b):
             if WARM_HEAD:
@@ -161,7 +167,7 @@ def tile_cursor_velocity_filter_d4_kernel(tc, x_bytes, x_scale, w, offset, gain,
             words = xw[k][:].bitcast(F32)
             banks["x", k] = [bank(b0 + t, f"xt{k}_{t}") for t in range(2)]
             for t in range(2):
-                turn(words[:, 512 * t : 512 * t + 512], banks["x", k][t])
+                turn(words[:, 512 * t : 512 * t + 512], banks["x", k][t], V_BLOCKS[2 * k + t] == 8)
 
         def take(engine, dst, b):
             src = b[:].rearrange("p (g u r) -> p g r u", g=2, u=2)
@@ -272,13 +278,17 @@ def tile_cursor_velocity_filter_d4_kernel(tc, x_bytes, x_scale, w, offset, gain,
         def quant_h(big):
             hc[big] = u32_tile(HALF, f"hc{big}")
             hsc[big] = u8_tile(HALF, f"hsc{big}")
-            nc.vector.quantize_mx(
-                out=hc[big][:].bitcast(FP8X4), scales=hsc[big][:], in_=hg[big][:].rearrange("p n t -> p (n t)")
-            )
+            parts = 2 if big == 7 else 1
+            n = HALF // parts
+            for i in range(parts):
+                c = slice(n * i, n * i + n)
+                nc.vector.quantize_mx(
+                    out=hc[big][:, c].bitcast(FP8X4), scales=hsc[big][:, c], in_=hg[big][:, c, :].rearrange("p n t -> p (n t)")
+                )
 
         acc = {}
-        where = {(0, 0): 4, (0, 1): 5, (0, 2): 6, (0, 3): 7, (0, 4): 0, (0, 5): 1, (0, 6): 4, (0, 7): 5,
-                 (1, 0): 6, (1, 1): 7, (1, 2): 0, (1, 3): 1, (1, 4): 4, (1, 5): 5, (1, 6): 2, (1, 7): 3}
+        where = {(0, 0): 6, (0, 1): 7, (0, 2): 4, (0, 3): 5, (0, 4): 0, (0, 5): 1, (0, 6): 6, (0, 7): 7,
+                 (1, 0): 4, (1, 1): 5, (1, 2): 0, (1, 3): 1, (1, 4): 6, (1, 5): 7, (1, 6): 2, (1, 7): 3}
 
         def second(h, pt, g):
             if g == 0:
@@ -303,6 +313,11 @@ def tile_cursor_velocity_filter_d4_kernel(tc, x_bytes, x_scale, w, offset, gain,
             nc.sync.dma_start(out=out[128 * pt : 128 * pt + 128, HALF * h : HALF * h + HALF], in_=res[:])
 
         widen(0)
+        nc.vector.tensor_copy(out=off_all[:, 0:HALF], in_=obs[0][:])
+        nc.scalar.copy(out=off_all[:, HALF:F], in_=obs[1][:])
+        nc.vector.tensor_copy(
+            out=gain_f[:].rearrange("p (g t) -> p g t", g=4), in_=gb[:, 0:16].rearrange("p (t g) -> p g t", t=4)
+        )
         make_og(0)
         turn_w(0, 0)
         empty_w(0, 0)
@@ -338,18 +353,18 @@ def tile_cursor_velocity_filter_d4_kernel(tc, x_bytes, x_scale, w, offset, gain,
             14: [(1, pt, 1) for pt in range(4)],
             15: [(1, pt, g) for pt in (4, 5) for g in range(2)],
             16: [(1, pt, 2) for pt in range(6)],
-            17: [(1, pt, g) for pt in (6, 7) for g in range(3)],
-            18: [(1, pt, 3) for pt in (0, 1, 2, 3, 4, 5, 6, 7)],
+            17: [(1, 6, 0), (1, 6, 1), (1, 6, 2), (1, 0, 3), (1, 1, 3), (1, 7, 0), (1, 2, 3), (1, 7, 1), (1, 3, 3), (1, 7, 2)]
+            + [(1, pt, 3) for pt in (4, 5, 6, 7)],
         }
 
-        for s in range(19):
+        for s in range(18):
             if s == 0:
                 first(0)
             if s + 2 < PAIRS:
                 turn_x(s + 2)
             if s - 1 in W_STEPS:
-                empty_w(s - 1 - W_STEPS[0] + 2, 0)
-                empty_w(s - 1 - W_STEPS[0] + 2, 1)
+                empty_w(s - 1, 0)
+                empty_w(s - 1, 1)
             if s + 3 < PAIRS:
                 widen(s + 3, 0)
             old = (s - 3) // 2
@@ -373,15 +388,18 @@ def tile_cursor_velocity_filter_d4_kernel(tc, x_bytes, x_scale, w, offset, gain,
                 quant_x(s + 1)
             if s in (5, 6):
                 quant_w(s - 3)
-            if s < 13:
+            if s < 5:
                 make_og(s + 3)
+            if 8 <= s + OG_LEAD < 16:
+                make_og(s + OG_LEAD)
             if 1 <= s < 16:
                 first(s)
             if s in W_STEPS:
-                turn_w(s - W_STEPS[0] + 2, 6 - 2 * (s - W_STEPS[0]))
+                turn_w(s, W_BANKS[s])
             if s == 17:
-                weave(7, 0, TAIL_COLS, "v")
+                weave(7, 0, 256, "v")
                 weave(7, TAIL_COLS, 512, "s")
+                weave(7, 256, TAIL_COLS, "v")
                 quant_h(7)
             for task in plan.get(s, []):
                 second(*task)

@@ -20,19 +20,40 @@ COPY = mybir.ActivationFunctionType.Copy
 
 HALF = 512
 PAIRS = 8
-V_BLOCKS = (8, 8, 8, 7, 7, 0, 2, 0, 3, 2, 8, 0, 6, 0, 3, 0)
-OG_ENGINES = "vvvvvvvssvsvssss"
-OUT_ENGINES = "ssssssssssssssss"
-X_ENGINES = "sssvsssssssssvss"
-W_ENGINES = "ssssssss"
-WEAVE_ENGINES = "vvvssssvvvvvvv"
-TAIL_COLS = 384
-OG_LEAD = 1
+GROUPS = 4
+SCALE_BLOCK = 128
+
 X_BANKS = (6, 4, 0, 4, 0, 4, 4, 0)
 W_BANKS = (0, 2, 6, 0)
-WARM = 10
-W_STEPS = (2, 3)
-WARM_HEAD = 2
+SUM_BANKS = ((6, 7, 4, 5, 0, 6, 7, 4), (5, 0, 6, 7, 4, 3, 1, 2))
+
+
+def vector_widens(i):
+    return i < 4 or i % 3 == 1
+
+
+def scalar_weaves(big, part):
+    return 3 <= 2 * big + part <= 6
+
+
+def second_product_plan():
+    plan = {s: [] for s in range(18)}
+    plan[4] = [(0, 0, 0), (0, 1, 0)]
+    plan[5] = [(0, 2, 0), (0, 3, 0)]
+    plan[6] = [(0, 0, 1), (0, 1, 1), (0, 4, 0), (0, 4, 1)]
+    plan[7] = [(0, 2, 1), (0, 3, 1)]
+    plan[8] = [(0, 0, 2), (0, 1, 2), (0, 2, 2)]
+    plan[9] = [(0, 3, 2), (0, 4, 2)]
+    plan[10] = [(0, tile, 3) for tile in range(5)]
+    for tile in (5, 6, 7):
+        plan[6 + tile] = [(0, tile, g) for g in range(GROUPS)]
+    plan[14] = [(1, tile, 0) for tile in range(4)]
+    plan[15] = [(1, tile, 1) for tile in range(4)]
+    plan[16] = [(1, 4, 0), (1, 4, 1)] + [(1, tile, 2) for tile in range(5)]
+    plan[17] = [(1, 5, 0), (1, 5, 1), (1, 5, 2), (1, 0, 3), (1, 1, 3)]
+    plan[17] += [(1, 6, 0), (1, 2, 3), (1, 6, 1), (1, 3, 3), (1, 6, 2), (1, 4, 3)]
+    plan[17] += [(1, 7, 0), (1, 5, 3), (1, 7, 1), (1, 6, 3), (1, 7, 2), (1, 7, 3)]
+    return plan
 
 
 def tile_cursor_velocity_filter_d4_kernel(tc, x_bytes, x_scale, w, offset, gain, filt_words, filt_scales, out):
@@ -40,7 +61,7 @@ def tile_cursor_velocity_filter_d4_kernel(tc, x_bytes, x_scale, w, offset, gain,
     with ExitStack() as ctx:
         keep = ctx.enter_context(tc.tile_pool(name="keep", bufs=1))
         work = ctx.enter_context(tc.tile_pool(name="work", bufs=3))
-        hwork = ctx.enter_context(tc.tile_pool(name="hwork", bufs=2))
+        h_work = ctx.enter_context(tc.tile_pool(name="h_work", bufs=2))
         stage = ctx.enter_context(tc.tile_pool(name="stage", bufs=10))
         psum = ctx.enter_context(tc.psum_pool(name="psum", bufs=1))
         ctx.enter_context(tc.manual_schedule())
@@ -48,360 +69,330 @@ def tile_cursor_velocity_filter_d4_kernel(tc, x_bytes, x_scale, w, offset, gain,
         def bank(i, name):
             return psum.tile([128, HALF], F32, name=name, tag=f"bank{i}")
 
-        def u32_tile(cols, name):
-            return keep.tile([128, cols], U32, name=name, align_bytes=64)
+        def kept(cols, dtype, name):
+            return keep.tile([128, cols], dtype, name=name, align_bytes=64)
 
-        def u8_tile(cols, name):
-            return keep.tile([128, cols], U8, name=name, align_bytes=64)
-
-        zeros = keep.tile([128, HALF], BF16, name="zeros")
+        zeros = kept(HALF, BF16, "zeros")
         nc.vector.memset(zeros[:], 0.0)
-        spare = bank(3, "spare")
-        off_row = keep.tile([128, F], BF16, name="off_row")
-        nc.vector.memset(off_row[:], 0.0)
-        ones = keep.tile([128, 128], BF16, name="ones")
+        offset_rows = kept(F, BF16, "offset_rows")
+        nc.vector.memset(offset_rows[:], 0.0)
+        ones = kept(128, BF16, "ones")
         nc.vector.memset(ones[:], 1.0)
-        ident = keep.tile([128, 128], F32, name="ident")
+        ident = kept(128, F32, "ident")
         make_identity(nc, ident[:])
-        fs = u8_tile(4 * P, "fs")
-        nc.gpsimd.memset(fs[:].bitcast(I32), 0)
-
-        gain_rows = keep.tile([128, 512], BF16, name="gain_rows")
+        filt_s = kept(GROUPS * P, U8, "filt_s")
+        nc.gpsimd.memset(filt_s[:].bitcast(I32), 0)
+        gain_rows = kept(512, BF16, "gain_rows")
         nc.vector.memset(gain_rows[:], 0.0)
-        nc.scalar.dma_start(out=off_row[0:1, :], in_=offset.unsqueeze(0))
+        nc.scalar.dma_start(out=offset_rows[0:1, :], in_=offset.unsqueeze(0))
         nc.scalar.dma_start(out=gain_rows[0:4, :], in_=gain.rearrange("(g c) -> g c", g=4))
 
-        xs = keep.tile([128, 4, 32], F32, name="xs")
-        xs_view = x_scale.rearrange("(g p t) j -> p g (t j)", p=128, t=4)
-        nc.sync.dma_start(out=xs[:, 0, :], in_=xs_view[:, 0, :])
-        x_view = x_bytes.rearrange("(g p t) k -> g p (t k)", p=128, t=4)
-        xb = [keep.tile([128, 4 * K], U8, name=f"xb{g}", align_bytes=64) for g in range(4)]
-        wr = [keep.tile([128, K], BF16, name=f"wr{r}", align_bytes=64) for r in range(8)]
+        x_s = keep.tile([128, GROUPS, 32], F32, name="x_s")
+        x_s_view = x_scale.rearrange("(g p t) j -> p g (t j)", p=128, t=4)
+        x_b = [kept(4 * K, U8, f"x_b{g}") for g in range(GROUPS)]
+        x_b_view = x_bytes.rearrange("(g p t) k -> g p (t k)", p=128, t=4)
+        w_rows = [kept(K, BF16, f"w_rows{r}") for r in range(8)]
 
         def load_w(r):
-            nc.sync.dma_start(out=wr[r][:], in_=w[128 * r : 128 * r + 128, :])
+            nc.sync.dma_start(out=w_rows[r][:], in_=w[128 * r : 128 * r + 128, :])
 
-        nc.sync.dma_start(out=xb[0][:, 0 : 2 * K], in_=x_view[0][:, 0 : 2 * K])
+        nc.sync.dma_start(out=x_s[:, 0, :], in_=x_s_view[:, 0, :])
+        nc.sync.dma_start(out=x_b[0][:, 0 : 2 * K], in_=x_b_view[0][:, 0 : 2 * K])
         load_w(0)
         load_w(1)
-        nc.sync.dma_start(out=xb[0][:, 2 * K : 4 * K], in_=x_view[0][:, 2 * K : 4 * K])
+        nc.sync.dma_start(out=x_b[0][:, 2 * K : 4 * K], in_=x_b_view[0][:, 2 * K : 4 * K])
         load_w(2)
         load_w(3)
-        nc.sync.dma_start(out=xs[:, 1:4, :], in_=xs_view[:, 1:4, :])
-        for g in range(1, 4):
-            nc.sync.dma_start(out=xb[g][:], in_=x_view[g])
+        nc.sync.dma_start(out=x_s[:, 1:GROUPS, :], in_=x_s_view[:, 1:GROUPS, :])
+        for g in range(1, GROUPS):
+            nc.sync.dma_start(out=x_b[g][:], in_=x_b_view[g])
         for r in range(4, 8):
             load_w(r)
-        fw = u8_tile(4 * 2 * P, "fw")
+        filt_w = kept(GROUPS * 2 * P, U8, "filt_w")
         nc.sync.dma_start(
-            out=fw[:].bitcast(I32).rearrange("p (g c) -> p g c", g=4),
+            out=filt_w[:].bitcast(I32).rearrange("p (g c) -> p g c", g=GROUPS),
             in_=filt_words.bitcast(I32).rearrange("g p c -> p g c"),
         )
         for q in range(4):
             nc.sync.dma_start(
-                out=fs[32 * q : 32 * q + 4, :].bitcast(I32).rearrange("q (g n) -> q g n", g=4),
+                out=filt_s[32 * q : 32 * q + 4, :].bitcast(I32).rearrange("q (g n) -> q g n", g=GROUPS),
                 in_=filt_scales.bitcast(I32)[:, 4 * q : 4 * q + 4, :].rearrange("g q n -> q g n"),
             )
 
-        gain_f = keep.tile([128, 16], F32, name="gain_f")
-        ident_bf = keep.tile([128, 4], BF16, name="ident_bf")
-        nc.vector.tensor_copy(out=ident_bf[:], in_=ident[:, 0:4])
+        pick = keep.tile([128, 4], BF16, name="pick")
+        nc.vector.tensor_copy(out=pick[:], in_=ident[:, 0:4])
 
-        for i in range(WARM):
-            nc.tensor.matmul(spare[:], lhsT=zeros[:, 0:128], rhs=zeros[:], start=True, stop=True)
+        def warm_up(i, count):
+            idle = bank(i, f"idle{i}")
+            for n in range(count):
+                nc.tensor.matmul(idle[:], lhsT=zeros[:, 0:128], rhs=zeros[:], start=True, stop=True)
 
-        off_all = keep.tile([128, F], BF16, name="off_all")
-        obs = []
-        for h in range(2):
-            ob = bank(4 + h, f"ob{h}")
-            nc.tensor.matmul(ob[:], lhsT=ones[:], rhs=off_row[:, HALF * h : HALF * h + HALF], start=True, stop=True)
-            obs.append(ob)
-        gb = bank(2, "gb")
+        warm_up(3, 10)
+
+        offset_banks = []
+        for half in range(2):
+            ob = bank(4 + half, f"offset_bank{half}")
+            nc.tensor.matmul(ob[:], lhsT=ones[:], rhs=offset_rows[:, HALF * half : HALF * half + HALF], start=True, stop=True)
+            offset_banks.append(ob)
+        gain_bank = bank(2, "gain_bank")
         for t in range(4):
-            nc.tensor.matmul(gb[:, 4 * t : 4 * t + 4], lhsT=gain_rows[:, t:512:4], rhs=ident_bf[:], start=True, stop=True)
+            nc.tensor.matmul(gain_bank[:, 4 * t : 4 * t + 4], lhsT=gain_rows[:, t:512:4], rhs=pick[:], start=True, stop=True)
+        offset_all = kept(F, BF16, "offset_all")
+        gain_all = keep.tile([128, 4 * GROUPS], F32, name="gain_all")
 
-        xw = {}
-        xg = {}
-        xc = {}
-        xsc = {}
-        banks = {}
-
-        def widen(k, part=None):
-            g, h = divmod(k, 2)
-            if part in (None, 0):
-                xw[k] = work.tile([128, 2 * K], BF16, name=f"xw{k}", tag="xw", align_bytes=64)
-            blocks = range(16) if part is None else range(8 * part, 8 * part + 8)
-            for b in blocks:
-                src = xb[g][:, 2 * K * h + 128 * b : 2 * K * h + 128 * b + 128].bitcast(FP8)
-                dst = xw[k][:, 128 * b : 128 * b + 128]
-                sc = xs[:, g, 16 * h + b : 16 * h + b + 1]
-                t, j = divmod(b, 8)
-                nv = V_BLOCKS[2 * k + t]
-                if nv == 8:
-                    by_u = xw[k][:, K * t : K * t + K].rearrange("x (g u p e) -> x g p u e", g=2, u=2, e=2)
-                    dst = by_u[:, j // 4, 32 * (j % 4) : 32 * (j % 4) + 32, :, :]
-                    src = src.rearrange("x (p u e) -> x p u e", u=2, e=2)
-                if (j + 1) * nv // 8 > j * nv // 8:
-                    nc.vector.tensor_scalar(out=dst, in0=src, scalar1=sc, scalar2=None, op0=MULT)
-                else:
-                    nc.scalar.activation(out=dst, in_=src, func=COPY, scale=sc)
-
-        def turn(words, b, by_u=False):
-            for g in range(2):
-                for u in range(2):
-                    c = 2 * g + u
-                    if by_u:
-                        part = words[:, 128 * c : 128 * c + 128]
-                    else:
-                        part = words[:, 256 * g + u : 256 * g + 256 : 2]
-                    nc.tensor.transpose(b[:, 128 * c : 128 * c + 128], part, ident[:])
-
-        def keep_warm(b):
-            if WARM_HEAD:
-                idle = bank(b, f"idle{b}")
-                for i in range(WARM_HEAD):
-                    nc.tensor.matmul(idle[:], lhsT=zeros[:, 0:128], rhs=zeros[:], start=True, stop=True)
-
-        def turn_x(k):
-            b0 = X_BANKS[k]
-            words = xw[k][:].bitcast(F32)
-            banks["x", k] = [bank(b0 + t, f"xt{k}_{t}") for t in range(2)]
-            for t in range(2):
-                turn(words[:, 512 * t : 512 * t + 512], banks["x", k][t], V_BLOCKS[2 * k + t] == 8)
-
-        def take(engine, dst, b):
-            src = b[:].rearrange("p (g u r) -> p g r u", g=2, u=2)
-            if engine == "s":
-                nc.scalar.copy(out=dst, in_=src)
-            else:
-                nc.vector.tensor_copy(out=dst, in_=src)
-
-        def empty_x(k, t):
-            if t == 0:
-                xg[k] = work.tile([128, 2, 2, 128, 4], BF16, name=f"xg{k}", tag="xg", align_bytes=64)
-            dst = xg[k][:].rearrange("p a g r v -> p (a g r v)").bitcast(F32)[:, 512 * t : 512 * t + 512]
-            take(X_ENGINES[2 * k + t], dst.rearrange("p (g r u) -> p g r u", g=2, u=2), banks["x", k][t])
-
-        def quant_x(k):
-            xc[k] = u32_tile(512, f"xc{k}")
-            xsc[k] = u8_tile(512, f"xsc{k}")
-            nc.vector.quantize_mx(
-                out=xc[k][:].bitcast(FP8X4), scales=xsc[k][:], in_=xg[k][:].rearrange("p a g r v -> p (a g r v)")
+        def spread_offset_and_gain():
+            nc.vector.tensor_copy(out=offset_all[:, 0:HALF], in_=offset_banks[0][:])
+            nc.scalar.copy(out=offset_all[:, HALF:F], in_=offset_banks[1][:])
+            nc.vector.tensor_copy(
+                out=gain_all[:].rearrange("p (g t) -> p g t", g=GROUPS),
+                in_=gain_bank[:, 0:16].rearrange("p (t g) -> p g t", t=4),
             )
 
-        wg = {}
-        wc = {}
-        wsc = {}
+        turned = {}
+        x_wide, x_in, x_codes, x_scales = {}, {}, {}, {}
 
-        def turn_w(j, b0):
-            banks["w", j] = [bank(b0 + t, f"wt{j}_{t}") for t in range(2)]
-            for t in range(2):
-                turn(wr[2 * j + t][:].bitcast(F32), banks["w", j][t])
-
-        def empty_w(j, t):
+        def widen(k, t):
             if t == 0:
-                wg[j] = work.tile([128, 2, 256, 4], BF16, name=f"wg{j}", tag="wg", bufs=2, align_bytes=64)
-            dst = wg[j][:].rearrange("p g r v -> p (g r v)").bitcast(F32).rearrange("p (g r u) -> p g r u", g=2, u=2)
-            take(W_ENGINES[2 * j + t], dst[:, :, 128 * t : 128 * t + 128, :], banks["w", j][t])
+                x_wide[k] = work.tile([128, 2 * K], BF16, name=f"x_wide{k}", tag="x_wide", align_bytes=64)
+            g, h = divmod(k, 2)
+            by_u = x_wide[k][:, K * t : K * t + K].rearrange("x (g u p e) -> x g p u e", g=2, u=2, e=2)
+            for j in range(8):
+                c = K * (2 * h + t) + SCALE_BLOCK * j
+                src = x_b[g][:, c : c + SCALE_BLOCK].bitcast(FP8)
+                scale = x_s[:, g, 8 * (2 * h + t) + j : 8 * (2 * h + t) + j + 1]
+                if vector_widens(2 * k + t):
+                    p0 = 32 * (j % 4)
+                    nc.vector.tensor_scalar(
+                        out=by_u[:, j // 4, p0 : p0 + 32, :, :],
+                        in0=src.rearrange("x (p u e) -> x p u e", u=2, e=2),
+                        scalar1=scale,
+                        scalar2=None,
+                        op0=MULT,
+                    )
+                else:
+                    c = K * t + SCALE_BLOCK * j
+                    nc.scalar.activation(out=x_wide[k][:, c : c + SCALE_BLOCK], in_=src, func=COPY, scale=scale)
 
-        def quant_w(j):
-            h, q = divmod(j, 2)
+        def turn(words, b, by_u):
+            for g in range(2):
+                for u in range(2):
+                    c = 128 * (2 * g + u)
+                    part = words[:, c : c + 128] if by_u else words[:, 256 * g + u : 256 * g + 256 : 2]
+                    nc.tensor.transpose(b[:, c : c + 128], part, ident[:])
+
+        def turn_x(k):
+            words = x_wide[k][:].bitcast(F32)
+            turned["x", k] = [bank(X_BANKS[k] + t, f"x_turned{k}_{t}") for t in range(2)]
+            for t in range(2):
+                turn(words[:, 512 * t : 512 * t + 512], turned["x", k][t], vector_widens(2 * k + t))
+
+        def turn_w(j):
+            turned["w", j] = [bank(W_BANKS[j] + t, f"w_turned{j}_{t}") for t in range(2)]
+            for t in range(2):
+                turn(w_rows[2 * j + t][:].bitcast(F32), turned["w", j][t], False)
+
+        def empty(copy, dst, b):
+            copy(out=dst, in_=b[:].rearrange("p (g u r) -> p g r u", g=2, u=2))
+
+        def empty_x(k, t, copy):
+            if t == 0:
+                x_in[k] = work.tile([128, 2, 2, 128, 4], BF16, name=f"x_in{k}", tag="x_in", align_bytes=64)
+            words = x_in[k][:].rearrange("p a g r v -> p (a g r v)").bitcast(F32)
+            empty(copy, words[:, 512 * t : 512 * t + 512].rearrange("p (g r u) -> p g r u", g=2, u=2), turned["x", k][t])
+
+        def quantise_x(k):
+            x_codes[k] = kept(512, U32, f"x_codes{k}")
+            x_scales[k] = kept(512, U8, f"x_scales{k}")
+            nc.vector.quantize_mx(
+                out=x_codes[k][:].bitcast(FP8X4),
+                scales=x_scales[k][:],
+                in_=x_in[k][:].rearrange("p a g r v -> p (a g r v)"),
+            )
+
+        w_in, w_codes, w_scales = {}, {}, {}
+
+        def empty_w(j, t, copy):
+            if t == 0:
+                w_in[j] = work.tile([128, 2, 256, 4], BF16, name=f"w_in{j}", tag="w_in", bufs=2, align_bytes=64)
+            words = w_in[j][:].rearrange("p g r v -> p (g r v)").bitcast(F32).rearrange("p (g r u) -> p g r u", g=2, u=2)
+            empty(copy, words[:, :, 128 * t : 128 * t + 128, :], turned["w", j][t])
+
+        def quantise_w(j):
+            half, q = divmod(j, 2)
             if q == 0:
-                wc[h] = u32_tile(2 * HALF, f"wc{h}")
-                wsc[h] = u8_tile(2 * HALF, f"wsc{h}")
+                w_codes[half] = kept(2 * HALF, U32, f"w_codes{half}")
+                w_scales[half] = kept(2 * HALF, U8, f"w_scales{half}")
             for g in range(2):
                 c = slice(HALF * g + 256 * q, HALF * g + 256 * q + 256)
                 nc.vector.quantize_mx(
-                    out=wc[h][:, c].bitcast(FP8X4), scales=wsc[h][:, c], in_=wg[j][:, g, :, :].rearrange("p r v -> p (r v)")
+                    out=w_codes[half][:, c].bitcast(FP8X4),
+                    scales=w_scales[half][:, c],
+                    in_=w_in[j][:, g, :, :].rearrange("p r v -> p (r v)"),
                 )
 
-        og = {}
-        hp = {}
-        hg = {}
-        hc = {}
-        hsc = {}
+        offset_gain, y_banks, h_planes, h_in, h_codes, h_scales = {}, {}, {}, {}, {}, {}
 
-        def make_og(m):
-            h, k = divmod(m, PAIRS)
-            og[m] = work.tile([128, 2, HALF], F32, name=f"og{m}", tag="og", bufs=10)
+        def scale_offset(m):
+            half, k = divmod(m, PAIRS)
+            offset_gain[m] = work.tile([128, 2, HALF], F32, name=f"offset_gain{m}", tag="offset_gain", bufs=10)
+            src = offset_all[:, HALF * half : HALF * half + HALF]
             for t in range(2):
-                i = 2 * k + t
-                src = off_all[:, HALF * h : HALF * h + HALF]
-                if OG_ENGINES[m] == "s":
-                    nc.scalar.activation(out=og[m][:, t, :], in_=src, func=COPY, scale=gain_f[:, i : i + 1])
+                g1 = gain_all[:, 2 * k + t : 2 * k + t + 1]
+                if half == 0:
+                    nc.vector.tensor_scalar(out=offset_gain[m][:, t, :], in0=src, scalar1=g1, scalar2=None, op0=MULT)
                 else:
-                    nc.vector.tensor_scalar(
-                        out=og[m][:, t, :], in0=src, scalar1=gain_f[:, i : i + 1], scalar2=None, op0=MULT
-                    )
+                    nc.scalar.activation(out=offset_gain[m][:, t, :], in_=src, func=COPY, scale=g1)
 
-        def first(m):
-            h, k = divmod(m, PAIRS)
-            banks["y", m] = [bank(2 + t, f"y{m}_{t}") for t in range(2)]
+        def multiply(m):
+            half, k = divmod(m, PAIRS)
+            y_banks[m] = [bank(2 + t if half == 0 else (2, 3, 1)[(2 * m + t) % 3], f"y{m}_{t}") for t in range(2)]
             for t in range(2):
                 for g in range(2):
-                    c = 128 * (2 * t + g)
+                    rows = slice(128 * (2 * t + g), 128 * (2 * t + g) + 128)
+                    cols = slice(HALF * g, HALF * g + HALF)
                     nc.tensor.matmul_mx(
-                        out=banks["y", m][t][:],
-                        lhsT=xc[k][:, c : c + 128].bitcast(FP8X4),
-                        lhsT_scale=xsc[k][:, c : c + 128],
-                        rhs=wc[h][:, HALF * g : HALF * g + HALF].bitcast(FP8X4),
-                        rhs_scale=wsc[h][:, HALF * g : HALF * g + HALF],
+                        out=y_banks[m][t][:],
+                        lhsT=x_codes[k][:, rows].bitcast(FP8X4),
+                        lhsT_scale=x_scales[k][:, rows],
+                        rhs=w_codes[half][:, cols].bitcast(FP8X4),
+                        rhs_scale=w_scales[half][:, cols],
                         start=(g == 0),
                         stop=(g == 1),
                     )
 
         def finish(m, t):
-            h, k = divmod(m, PAIRS)
+            k = m % PAIRS
             big, q = divmod(m, 2)
             if q == 0 and t == 0:
-                hp[big] = hwork.tile([128, 4, HALF], BF16, name=f"hp{big}", tag="hp", align_bytes=64)
-            i = 2 * k + t
+                h_planes[big] = h_work.tile([128, 4, HALF], BF16, name=f"h_planes{big}", tag="h_planes", align_bytes=64)
             nc.vector.scalar_tensor_tensor(
-                out=hp[big][:, 2 * q + t, :],
-                in0=banks["y", m][t][:],
-                scalar=gain_f[:, i : i + 1],
-                in1=og[m][:, t, :],
+                out=h_planes[big][:, 2 * q + t, :],
+                in0=y_banks[m][t][:],
+                scalar=gain_all[:, 2 * k + t : 2 * k + t + 1],
+                in1=offset_gain[m][:, t, :],
                 op0=MULT,
                 op1=ADD,
             )
 
-        def weave(big, first_col, last_col, engine):
-            if first_col == 0:
-                hg[big] = hwork.tile([128, HALF, 4], BF16, name=f"hg{big}", tag="hg", align_bytes=64)
-            c = slice(first_col, last_col)
-            dst, src = hg[big][:, c, :], hp[big][:, :, c].rearrange("p t n -> p n t")
-            if engine == "s":
-                nc.scalar.copy(out=dst, in_=src)
-            else:
-                nc.vector.tensor_copy(out=dst, in_=src)
+        def weave(big, first, last, copy):
+            if first == 0:
+                h_in[big] = h_work.tile([128, HALF, 4], BF16, name=f"h_in{big}", tag="h_in", align_bytes=64)
+            copy(
+                out=h_in[big][:, first:last, :].rearrange("p (c i) t -> p c t i", i=4),
+                in_=h_planes[big][:, :, first:last].rearrange("p t (c i) -> p c t i", i=4),
+            )
 
-        def quant_h(big):
-            hc[big] = u32_tile(HALF, f"hc{big}")
-            hsc[big] = u8_tile(HALF, f"hsc{big}")
-            parts = 2 if big == 7 else 1
+        def quantise_h(big, parts):
+            h_codes[big] = kept(HALF, U32, f"h_codes{big}")
+            h_scales[big] = kept(HALF, U8, f"h_scales{big}")
             n = HALF // parts
             for i in range(parts):
                 c = slice(n * i, n * i + n)
                 nc.vector.quantize_mx(
-                    out=hc[big][:, c].bitcast(FP8X4), scales=hsc[big][:, c], in_=hg[big][:, c, :].rearrange("p n t -> p (n t)")
+                    out=h_codes[big][:, c].bitcast(FP8X4),
+                    scales=h_scales[big][:, c],
+                    in_=h_in[big][:, c, :].rearrange("p n t -> p (n t)"),
                 )
 
-        acc = {}
-        where = {(0, 0): 6, (0, 1): 7, (0, 2): 4, (0, 3): 5, (0, 4): 0, (0, 5): 1, (0, 6): 6, (0, 7): 7,
-                 (1, 0): 4, (1, 1): 5, (1, 2): 0, (1, 3): 1, (1, 4): 6, (1, 5): 7, (1, 6): 2, (1, 7): 3}
+        sums = {}
 
-        def second(h, pt, g):
+        def filter_pass(half, tile, g):
             if g == 0:
-                acc[h, pt] = bank(where[h, pt], f"acc{h}_{pt}")
-            big = 4 * h + g
+                sums[half, tile] = bank(SUM_BANKS[half][tile], f"sum{half}_{tile}")
+            big = GROUPS * half + g
+            words = slice(2 * P * g + 256 * tile, 2 * P * g + 256 * tile + 256)
+            scales = slice(P * g + 128 * tile, P * g + 128 * tile + 128)
             nc.tensor.matmul_mx(
-                out=acc[h, pt][:],
-                lhsT=fw[:, 2 * P * g + 256 * pt : 2 * P * g + 256 * pt + 256].bitcast(FP4X4),
-                lhsT_scale=fs[:, P * g + 128 * pt : P * g + 128 * pt + 128],
-                rhs=hc[big][:].bitcast(FP8X4),
-                rhs_scale=hsc[big][:],
+                out=sums[half, tile][:],
+                lhsT=filt_w[:, words].bitcast(FP4X4),
+                lhsT_scale=filt_s[:, scales],
+                rhs=h_codes[big][:].bitcast(FP8X4),
+                rhs_scale=h_scales[big][:],
                 start=(g == 0),
-                stop=(g == 3),
+                stop=(g == GROUPS - 1),
             )
 
-        def store(h, pt):
-            res = stage.tile([128, HALF], F32, name=f"res{h}_{pt}", tag="res")
-            if OUT_ENGINES[8 * h + pt] == "s":
-                nc.scalar.copy(out=res[:], in_=acc[h, pt][:])
-            else:
-                nc.vector.tensor_copy(out=res[:], in_=acc[h, pt][:])
-            nc.sync.dma_start(out=out[128 * pt : 128 * pt + 128, HALF * h : HALF * h + HALF], in_=res[:])
+        def store(half, tile):
+            result = stage.tile([128, HALF], F32, name=f"result{half}_{tile}", tag="result")
+            nc.scalar.copy(out=result[:], in_=sums[half, tile][:])
+            nc.sync.dma_start(out=out[128 * tile : 128 * tile + 128, HALF * half : HALF * half + HALF], in_=result[:])
 
-        widen(0)
-        nc.vector.tensor_copy(out=off_all[:, 0:HALF], in_=obs[0][:])
-        nc.scalar.copy(out=off_all[:, HALF:F], in_=obs[1][:])
-        nc.vector.tensor_copy(
-            out=gain_f[:].rearrange("p (g t) -> p g t", g=4), in_=gb[:, 0:16].rearrange("p (t g) -> p g t", t=4)
-        )
-        make_og(0)
-        turn_w(0, 0)
-        empty_w(0, 0)
-        empty_w(0, 1)
+        vector_copy, scalar_copy = nc.vector.tensor_copy, nc.scalar.copy
+
+        widen(0, 0)
+        widen(0, 1)
+        spread_offset_and_gain()
+        scale_offset(0)
+        turn_w(0)
+        empty_w(0, 0, scalar_copy)
+        empty_w(0, 1, scalar_copy)
         turn_x(0)
-        quant_w(0)
-        keep_warm(5)
-        turn_w(1, 2)
-        empty_x(0, 0)
-        empty_x(0, 1)
+        quantise_w(0)
+        warm_up(5, 2)
+        turn_w(1)
+        empty_x(0, 0, scalar_copy)
+        empty_x(0, 1, scalar_copy)
         widen(1, 0)
-        empty_w(1, 0)
-        empty_w(1, 1)
-        quant_x(0)
+        empty_w(1, 0, scalar_copy)
+        empty_w(1, 1, scalar_copy)
+        quantise_x(0)
         widen(1, 1)
-        quant_w(1)
+        quantise_w(1)
         turn_x(1)
-        make_og(1)
-        empty_x(1, 0)
-        empty_x(1, 1)
-        widen(2)
-        make_og(2)
+        scale_offset(1)
+        empty_x(1, 0, scalar_copy)
+        empty_x(1, 1, vector_copy)
+        widen(2, 0)
+        widen(2, 1)
+        scale_offset(2)
 
-        plan = {
-            4: [(0, 0, 0), (0, 1, 0)], 5: [(0, 2, 0), (0, 3, 0)],
-            6: [(0, 0, 1), (0, 1, 1), (0, 4, 0), (0, 4, 1)], 7: [(0, 2, 1), (0, 3, 1), (0, 5, 0), (0, 5, 1)],
-            8: [(0, 0, 2), (0, 1, 2), (0, 2, 2)],
-            9: [(0, 3, 2), (0, 4, 2), (0, 5, 2)],
-            10: [(0, pt, 3) for pt in range(6)],
-            11: [(0, 6, g) for g in range(4)],
-            12: [(0, 7, g) for g in range(4)],
-            13: [(1, pt, 0) for pt in range(4)],
-            14: [(1, pt, 1) for pt in range(4)],
-            15: [(1, pt, g) for pt in (4, 5) for g in range(2)],
-            16: [(1, pt, 2) for pt in range(6)],
-            17: [(1, 6, 0), (1, 6, 1), (1, 6, 2), (1, 0, 3), (1, 1, 3), (1, 7, 0), (1, 2, 3), (1, 7, 1), (1, 3, 3), (1, 7, 2)]
-            + [(1, pt, 3) for pt in (4, 5, 6, 7)],
-        }
-
+        plan = second_product_plan()
         for s in range(18):
             if s == 0:
-                first(0)
+                multiply(0)
             if s + 2 < PAIRS:
                 turn_x(s + 2)
-            if s - 1 in W_STEPS:
-                empty_w(s - 1, 0)
-                empty_w(s - 1, 1)
+            if s - 1 in (2, 3):
+                empty_w(s - 1, 0, scalar_copy)
+                empty_w(s - 1, 1, scalar_copy)
             if s + 3 < PAIRS:
                 widen(s + 3, 0)
             old = (s - 3) // 2
+            interleaves = s % 2 == 1 and 0 <= old < 7
             if 1 <= s <= 16:
                 finish(s - 1, 0)
-            if s % 2 == 0 and s >= 4 and s < 18:
-                quant_h((s - 4) // 2)
-            if s % 2 == 1 and 3 <= s < 17:
-                weave(old, 0, 256, WEAVE_ENGINES[2 * old])
+            if s % 2 == 0 and s >= 4:
+                quantise_h((s - 4) // 2, 1)
+            if interleaves:
+                weave(old, 0, 256, scalar_copy if scalar_weaves(old, 0) else vector_copy)
             if 1 <= s <= 16:
                 finish(s - 1, 1)
-            if s % 2 == 1 and 3 <= s < 17:
-                weave(old, 256, 512, WEAVE_ENGINES[2 * old + 1])
+            if interleaves:
+                weave(old, 256, HALF, scalar_copy if scalar_weaves(old, 1) else vector_copy)
             if s + 2 < PAIRS:
-                empty_x(s + 2, 0)
+                empty_x(s + 2, 0, scalar_copy)
             if s + 3 < PAIRS:
                 widen(s + 3, 1)
             if s + 2 < PAIRS:
-                empty_x(s + 2, 1)
+                empty_x(s + 2, 1, scalar_copy)
             if s + 1 < PAIRS:
-                quant_x(s + 1)
+                quantise_x(s + 1)
             if s in (5, 6):
-                quant_w(s - 3)
-            if s < 5:
-                make_og(s + 3)
-            if 8 <= s + OG_LEAD < 16:
-                make_og(s + OG_LEAD)
-            if 1 <= s < 16:
-                first(s)
-            if s in W_STEPS:
-                turn_w(s, W_BANKS[s])
+                quantise_w(s - 3)
+            if s + 3 < PAIRS:
+                scale_offset(s + 3)
+            if PAIRS <= s + 1 < 2 * PAIRS:
+                scale_offset(s + 1)
+            if 1 <= s < 2 * PAIRS:
+                multiply(s)
+            if s in (2, 3):
+                turn_w(s)
             if s == 17:
-                weave(7, 0, 256, "v")
-                weave(7, TAIL_COLS, 512, "s")
-                weave(7, 256, TAIL_COLS, "v")
-                quant_h(7)
-            for task in plan.get(s, []):
-                second(*task)
-                if task[2] == 3:
-                    store(task[0], task[1])
+                weave(7, 0, 256, vector_copy)
+                weave(7, 384, HALF, scalar_copy)
+                weave(7, 256, 384, vector_copy)
+                quantise_h(7, 2)
+            for half, tile, g in plan[s]:
+                filter_pass(half, tile, g)
+                if g == GROUPS - 1:
+                    store(half, tile)

from contextlib import ExitStack

import concourse.mybir as mybir
from concourse.masks import make_identity

T, K, F, P = 2048, 1024, 1024, 1024
FLOPS = 2 * T * K * F + 2 * T * P * F

F32 = mybir.dt.float32
BF16 = mybir.dt.bfloat16
I32 = mybir.dt.int32
U32 = mybir.dt.uint32
U8 = mybir.dt.uint8
FP8 = mybir.dt.float8_e4m3fn
FP8X4 = mybir.dt.float8_e4m3fn_x4
FP4X4 = mybir.dt.float4_e2m1fn_x4
MULT = mybir.AluOpType.mult
ADD = mybir.AluOpType.add
COPY = mybir.ActivationFunctionType.Copy

HALF = 512
PAIRS = 8
GROUPS = 4
SCALE_BLOCK = 128

X_BANKS = (6, 4, 0, 4, 0, 4, 4, 0)
W_BANKS = (0, 2, 6, 0)
SUM_BANKS = ((6, 7, 4, 5, 0, 6, 7, 4), (5, 0, 6, 7, 4, 3, 1, 2))


def vector_widens(i):
    return i < 4 or i % 3 == 1


def scalar_weaves(big, part):
    return 3 <= 2 * big + part <= 6


def second_product_plan():
    plan = {s: [] for s in range(18)}
    plan[4] = [(0, 0, 0), (0, 1, 0)]
    plan[5] = [(0, 2, 0), (0, 3, 0)]
    plan[6] = [(0, 0, 1), (0, 1, 1), (0, 4, 0), (0, 4, 1)]
    plan[7] = [(0, 2, 1), (0, 3, 1)]
    plan[8] = [(0, 0, 2), (0, 1, 2), (0, 2, 2)]
    plan[9] = [(0, 3, 2), (0, 4, 2)]
    plan[10] = [(0, tile, 3) for tile in range(5)]
    for tile in (5, 6, 7):
        plan[6 + tile] = [(0, tile, g) for g in range(GROUPS)]
    plan[14] = [(1, tile, 0) for tile in range(4)]
    plan[15] = [(1, tile, 1) for tile in range(4)]
    plan[16] = [(1, 4, 0), (1, 4, 1)] + [(1, tile, 2) for tile in range(5)]
    plan[17] = [(1, 5, 0), (1, 5, 1), (1, 5, 2), (1, 0, 3), (1, 1, 3)]
    plan[17] += [(1, 6, 0), (1, 2, 3), (1, 6, 1), (1, 3, 3), (1, 6, 2), (1, 4, 3)]
    plan[17] += [(1, 7, 0), (1, 5, 3), (1, 7, 1), (1, 6, 3), (1, 7, 2), (1, 7, 3)]
    return plan


def tile_cursor_velocity_filter_d4_kernel(tc, x_bytes, x_scale, w, offset, gain, filt_words, filt_scales, out):
    nc = tc.nc
    with ExitStack() as ctx:
        keep = ctx.enter_context(tc.tile_pool(name="keep", bufs=1))
        work = ctx.enter_context(tc.tile_pool(name="work", bufs=3))
        h_work = ctx.enter_context(tc.tile_pool(name="h_work", bufs=2))
        stage = ctx.enter_context(tc.tile_pool(name="stage", bufs=10))
        psum = ctx.enter_context(tc.psum_pool(name="psum", bufs=1))
        ctx.enter_context(tc.manual_schedule())

        def bank(i, name):
            return psum.tile([128, HALF], F32, name=name, tag=f"bank{i}")

        def kept(cols, dtype, name):
            return keep.tile([128, cols], dtype, name=name, align_bytes=64)

        zeros = kept(HALF, BF16, "zeros")
        nc.vector.memset(zeros[:], 0.0)
        offset_rows = kept(F, BF16, "offset_rows")
        nc.vector.memset(offset_rows[:], 0.0)
        ones = kept(128, BF16, "ones")
        nc.vector.memset(ones[:], 1.0)
        ident = kept(128, F32, "ident")
        make_identity(nc, ident[:])
        filt_s = kept(GROUPS * P, U8, "filt_s")
        nc.gpsimd.memset(filt_s[:].bitcast(I32), 0)
        gain_rows = kept(512, BF16, "gain_rows")
        nc.vector.memset(gain_rows[:], 0.0)
        nc.scalar.dma_start(out=offset_rows[0:1, :], in_=offset.unsqueeze(0))
        nc.scalar.dma_start(out=gain_rows[0:4, :], in_=gain.rearrange("(g c) -> g c", g=4))

        x_s = keep.tile([128, GROUPS, 32], F32, name="x_s")
        x_s_view = x_scale.rearrange("(g p t) j -> p g (t j)", p=128, t=4)
        x_b = [kept(4 * K, U8, f"x_b{g}") for g in range(GROUPS)]
        x_b_view = x_bytes.rearrange("(g p t) k -> g p (t k)", p=128, t=4)
        w_rows = [kept(K, BF16, f"w_rows{r}") for r in range(8)]

        def load_w(r):
            nc.sync.dma_start(out=w_rows[r][:], in_=w[128 * r : 128 * r + 128, :])

        nc.sync.dma_start(out=x_s[:, 0, :], in_=x_s_view[:, 0, :])
        nc.sync.dma_start(out=x_b[0][:, 0 : 2 * K], in_=x_b_view[0][:, 0 : 2 * K])
        load_w(0)
        load_w(1)
        nc.sync.dma_start(out=x_b[0][:, 2 * K : 4 * K], in_=x_b_view[0][:, 2 * K : 4 * K])
        load_w(2)
        load_w(3)
        nc.sync.dma_start(out=x_s[:, 1:GROUPS, :], in_=x_s_view[:, 1:GROUPS, :])
        for g in range(1, GROUPS):
            nc.sync.dma_start(out=x_b[g][:], in_=x_b_view[g])
        for r in range(4, 8):
            load_w(r)
        filt_w = kept(GROUPS * 2 * P, U8, "filt_w")
        nc.sync.dma_start(
            out=filt_w[:].bitcast(I32).rearrange("p (g c) -> p g c", g=GROUPS),
            in_=filt_words.bitcast(I32).rearrange("g p c -> p g c"),
        )
        for q in range(4):
            nc.sync.dma_start(
                out=filt_s[32 * q : 32 * q + 4, :].bitcast(I32).rearrange("q (g n) -> q g n", g=GROUPS),
                in_=filt_scales.bitcast(I32)[:, 4 * q : 4 * q + 4, :].rearrange("g q n -> q g n"),
            )

        pick = keep.tile([128, 4], BF16, name="pick")
        nc.vector.tensor_copy(out=pick[:], in_=ident[:, 0:4])

        def warm_up(i, count):
            idle = bank(i, f"idle{i}")
            for n in range(count):
                nc.tensor.matmul(idle[:], lhsT=zeros[:, 0:128], rhs=zeros[:], start=True, stop=True)

        warm_up(3, 10)

        offset_banks = []
        for half in range(2):
            ob = bank(4 + half, f"offset_bank{half}")
            nc.tensor.matmul(ob[:], lhsT=ones[:], rhs=offset_rows[:, HALF * half : HALF * half + HALF], start=True, stop=True)
            offset_banks.append(ob)
        gain_bank = bank(2, "gain_bank")
        for t in range(4):
            nc.tensor.matmul(gain_bank[:, 4 * t : 4 * t + 4], lhsT=gain_rows[:, t:512:4], rhs=pick[:], start=True, stop=True)
        offset_all = kept(F, BF16, "offset_all")
        gain_all = keep.tile([128, 4 * GROUPS], F32, name="gain_all")

        def spread_offset_and_gain():
            nc.vector.tensor_copy(out=offset_all[:, 0:HALF], in_=offset_banks[0][:])
            nc.scalar.copy(out=offset_all[:, HALF:F], in_=offset_banks[1][:])
            nc.vector.tensor_copy(
                out=gain_all[:].rearrange("p (g t) -> p g t", g=GROUPS),
                in_=gain_bank[:, 0:16].rearrange("p (t g) -> p g t", t=4),
            )

        turned = {}
        x_wide, x_in, x_codes, x_scales = {}, {}, {}, {}

        def widen(k, t):
            if t == 0:
                x_wide[k] = work.tile([128, 2 * K], BF16, name=f"x_wide{k}", tag="x_wide", align_bytes=64)
            g, h = divmod(k, 2)
            by_u = x_wide[k][:, K * t : K * t + K].rearrange("x (g u p e) -> x g p u e", g=2, u=2, e=2)
            for j in range(8):
                c = K * (2 * h + t) + SCALE_BLOCK * j
                src = x_b[g][:, c : c + SCALE_BLOCK].bitcast(FP8)
                scale = x_s[:, g, 8 * (2 * h + t) + j : 8 * (2 * h + t) + j + 1]
                if vector_widens(2 * k + t):
                    p0 = 32 * (j % 4)
                    nc.vector.tensor_scalar(
                        out=by_u[:, j // 4, p0 : p0 + 32, :, :],
                        in0=src.rearrange("x (p u e) -> x p u e", u=2, e=2),
                        scalar1=scale,
                        scalar2=None,
                        op0=MULT,
                    )
                else:
                    c = K * t + SCALE_BLOCK * j
                    nc.scalar.activation(out=x_wide[k][:, c : c + SCALE_BLOCK], in_=src, func=COPY, scale=scale)

        def turn(words, b, by_u):
            for g in range(2):
                for u in range(2):
                    c = 128 * (2 * g + u)
                    part = words[:, c : c + 128] if by_u else words[:, 256 * g + u : 256 * g + 256 : 2]
                    nc.tensor.transpose(b[:, c : c + 128], part, ident[:])

        def turn_x(k):
            words = x_wide[k][:].bitcast(F32)
            turned["x", k] = [bank(X_BANKS[k] + t, f"x_turned{k}_{t}") for t in range(2)]
            for t in range(2):
                turn(words[:, 512 * t : 512 * t + 512], turned["x", k][t], vector_widens(2 * k + t))

        def turn_w(j):
            turned["w", j] = [bank(W_BANKS[j] + t, f"w_turned{j}_{t}") for t in range(2)]
            for t in range(2):
                turn(w_rows[2 * j + t][:].bitcast(F32), turned["w", j][t], False)

        def empty(copy, dst, b):
            copy(out=dst, in_=b[:].rearrange("p (g u r) -> p g r u", g=2, u=2))

        def empty_x(k, t, copy):
            if t == 0:
                x_in[k] = work.tile([128, 2, 2, 128, 4], BF16, name=f"x_in{k}", tag="x_in", align_bytes=64)
            words = x_in[k][:].rearrange("p a g r v -> p (a g r v)").bitcast(F32)
            empty(copy, words[:, 512 * t : 512 * t + 512].rearrange("p (g r u) -> p g r u", g=2, u=2), turned["x", k][t])

        def quantise_x(k):
            x_codes[k] = kept(512, U32, f"x_codes{k}")
            x_scales[k] = kept(512, U8, f"x_scales{k}")
            nc.vector.quantize_mx(
                out=x_codes[k][:].bitcast(FP8X4),
                scales=x_scales[k][:],
                in_=x_in[k][:].rearrange("p a g r v -> p (a g r v)"),
            )

        w_in, w_codes, w_scales = {}, {}, {}

        def empty_w(j, t, copy):
            if t == 0:
                w_in[j] = work.tile([128, 2, 256, 4], BF16, name=f"w_in{j}", tag="w_in", bufs=2, align_bytes=64)
            words = w_in[j][:].rearrange("p g r v -> p (g r v)").bitcast(F32).rearrange("p (g r u) -> p g r u", g=2, u=2)
            empty(copy, words[:, :, 128 * t : 128 * t + 128, :], turned["w", j][t])

        def quantise_w(j):
            half, q = divmod(j, 2)
            if q == 0:
                w_codes[half] = kept(2 * HALF, U32, f"w_codes{half}")
                w_scales[half] = kept(2 * HALF, U8, f"w_scales{half}")
            for g in range(2):
                c = slice(HALF * g + 256 * q, HALF * g + 256 * q + 256)
                nc.vector.quantize_mx(
                    out=w_codes[half][:, c].bitcast(FP8X4),
                    scales=w_scales[half][:, c],
                    in_=w_in[j][:, g, :, :].rearrange("p r v -> p (r v)"),
                )

        offset_gain, y_banks, h_planes, h_in, h_codes, h_scales = {}, {}, {}, {}, {}, {}

        def scale_offset(m):
            half, k = divmod(m, PAIRS)
            offset_gain[m] = work.tile([128, 2, HALF], F32, name=f"offset_gain{m}", tag="offset_gain", bufs=10)
            src = offset_all[:, HALF * half : HALF * half + HALF]
            for t in range(2):
                g1 = gain_all[:, 2 * k + t : 2 * k + t + 1]
                if half == 0:
                    nc.vector.tensor_scalar(out=offset_gain[m][:, t, :], in0=src, scalar1=g1, scalar2=None, op0=MULT)
                else:
                    nc.scalar.activation(out=offset_gain[m][:, t, :], in_=src, func=COPY, scale=g1)

        def multiply(m):
            half, k = divmod(m, PAIRS)
            y_banks[m] = [bank(2 + t if half == 0 else (2, 3, 1)[(2 * m + t) % 3], f"y{m}_{t}") for t in range(2)]
            for t in range(2):
                for g in range(2):
                    rows = slice(128 * (2 * t + g), 128 * (2 * t + g) + 128)
                    cols = slice(HALF * g, HALF * g + HALF)
                    nc.tensor.matmul_mx(
                        out=y_banks[m][t][:],
                        lhsT=x_codes[k][:, rows].bitcast(FP8X4),
                        lhsT_scale=x_scales[k][:, rows],
                        rhs=w_codes[half][:, cols].bitcast(FP8X4),
                        rhs_scale=w_scales[half][:, cols],
                        start=(g == 0),
                        stop=(g == 1),
                    )

        def finish(m, t):
            k = m % PAIRS
            big, q = divmod(m, 2)
            if q == 0 and t == 0:
                h_planes[big] = h_work.tile([128, 4, HALF], BF16, name=f"h_planes{big}", tag="h_planes", align_bytes=64)
            nc.vector.scalar_tensor_tensor(
                out=h_planes[big][:, 2 * q + t, :],
                in0=y_banks[m][t][:],
                scalar=gain_all[:, 2 * k + t : 2 * k + t + 1],
                in1=offset_gain[m][:, t, :],
                op0=MULT,
                op1=ADD,
            )

        def weave(big, first, last, copy):
            if first == 0:
                h_in[big] = h_work.tile([128, HALF, 4], BF16, name=f"h_in{big}", tag="h_in", align_bytes=64)
            copy(
                out=h_in[big][:, first:last, :].rearrange("p (c i) t -> p c t i", i=4),
                in_=h_planes[big][:, :, first:last].rearrange("p t (c i) -> p c t i", i=4),
            )

        def quantise_h(big, parts):
            h_codes[big] = kept(HALF, U32, f"h_codes{big}")
            h_scales[big] = kept(HALF, U8, f"h_scales{big}")
            n = HALF // parts
            for i in range(parts):
                c = slice(n * i, n * i + n)
                nc.vector.quantize_mx(
                    out=h_codes[big][:, c].bitcast(FP8X4),
                    scales=h_scales[big][:, c],
                    in_=h_in[big][:, c, :].rearrange("p n t -> p (n t)"),
                )

        sums = {}

        def filter_pass(half, tile, g):
            if g == 0:
                sums[half, tile] = bank(SUM_BANKS[half][tile], f"sum{half}_{tile}")
            big = GROUPS * half + g
            words = slice(2 * P * g + 256 * tile, 2 * P * g + 256 * tile + 256)
            scales = slice(P * g + 128 * tile, P * g + 128 * tile + 128)
            nc.tensor.matmul_mx(
                out=sums[half, tile][:],
                lhsT=filt_w[:, words].bitcast(FP4X4),
                lhsT_scale=filt_s[:, scales],
                rhs=h_codes[big][:].bitcast(FP8X4),
                rhs_scale=h_scales[big][:],
                start=(g == 0),
                stop=(g == GROUPS - 1),
            )

        def store(half, tile):
            result = stage.tile([128, HALF], F32, name=f"result{half}_{tile}", tag="result")
            nc.scalar.copy(out=result[:], in_=sums[half, tile][:])
            nc.sync.dma_start(out=out[128 * tile : 128 * tile + 128, HALF * half : HALF * half + HALF], in_=result[:])

        vector_copy, scalar_copy = nc.vector.tensor_copy, nc.scalar.copy

        widen(0, 0)
        widen(0, 1)
        spread_offset_and_gain()
        scale_offset(0)
        turn_w(0)
        empty_w(0, 0, scalar_copy)
        empty_w(0, 1, scalar_copy)
        turn_x(0)
        quantise_w(0)
        warm_up(5, 2)
        turn_w(1)
        empty_x(0, 0, scalar_copy)
        empty_x(0, 1, scalar_copy)
        widen(1, 0)
        empty_w(1, 0, scalar_copy)
        empty_w(1, 1, scalar_copy)
        quantise_x(0)
        widen(1, 1)
        quantise_w(1)
        turn_x(1)
        scale_offset(1)
        empty_x(1, 0, scalar_copy)
        empty_x(1, 1, vector_copy)
        widen(2, 0)
        widen(2, 1)
        scale_offset(2)

        plan = second_product_plan()
        for s in range(18):
            if s == 0:
                multiply(0)
            if s + 2 < PAIRS:
                turn_x(s + 2)
            if s - 1 in (2, 3):
                empty_w(s - 1, 0, scalar_copy)
                empty_w(s - 1, 1, scalar_copy)
            if s + 3 < PAIRS:
                widen(s + 3, 0)
            old = (s - 3) // 2
            interleaves = s % 2 == 1 and 0 <= old < 7
            if 1 <= s <= 16:
                finish(s - 1, 0)
            if s % 2 == 0 and s >= 4:
                quantise_h((s - 4) // 2, 1)
            if interleaves:
                weave(old, 0, 256, scalar_copy if scalar_weaves(old, 0) else vector_copy)
            if 1 <= s <= 16:
                finish(s - 1, 1)
            if interleaves:
                weave(old, 256, HALF, scalar_copy if scalar_weaves(old, 1) else vector_copy)
            if s + 2 < PAIRS:
                empty_x(s + 2, 0, scalar_copy)
            if s + 3 < PAIRS:
                widen(s + 3, 1)
            if s + 2 < PAIRS:
                empty_x(s + 2, 1, scalar_copy)
            if s + 1 < PAIRS:
                quantise_x(s + 1)
            if s in (5, 6):
                quantise_w(s - 3)
            if s + 3 < PAIRS:
                scale_offset(s + 3)
            if PAIRS <= s + 1 < 2 * PAIRS:
                scale_offset(s + 1)
            if 1 <= s < 2 * PAIRS:
                multiply(s)
            if s in (2, 3):
                turn_w(s)
            if s == 17:
                weave(7, 0, 256, vector_copy)
                weave(7, 384, HALF, scalar_copy)
                weave(7, 256, 384, vector_copy)
                quantise_h(7, 2)
            for half, tile, g in plan[s]:
                filter_pass(half, tile, g)
                if g == GROUPS - 1:
                    store(half, tile)
